import numpy as np
import ml_dtypes


def mxq(x, axis, fmt="e4m3"):
    dtype, down = {"e4m3": (ml_dtypes.float8_e4m3fn, 7), "e5m2": (ml_dtypes.float8_e5m2, 14)}[fmt]
    v = np.moveaxis(np.asarray(x, np.float32).astype(ml_dtypes.bfloat16).astype(np.float64), axis, -1)
    blocks = v.reshape(v.shape[:-1] + (-1, 32))
    amax = np.abs(blocks).max(-1, keepdims=True)
    byte = np.maximum(np.where(amax > 0, np.frexp(amax)[1] - 1 + 127, 0) - down, 1)
    scale = np.exp2(byte - 127.0)
    codes = (blocks / scale).astype(np.float32).astype(dtype).astype(np.float64)
    return np.moveaxis((codes * scale).reshape(v.shape), -1, axis)


WIDE = False


def mx_kscale(k):
    if not WIDE:
        return np.ones(k)
    levels = np.array([10, -10, 5, -5, 0])
    if k % 512:
        return np.exp2(np.random.permutation(np.resize(levels, k // 32))).repeat(32)
    a = np.empty((k // 512, 16))
    for p in range(k // 512):
        a[p, :8] = np.random.permutation(np.resize(levels, 8))
        for g in range(8):
            far = levels[np.abs(levels - a[p, g]) >= 10]
            a[p, g + 8] = far[np.random.randint(len(far))]
    return np.exp2(a.ravel()).repeat(32)


def f64(x):
    return np.asarray(x).astype(np.float64)


def striped(idx):
    return np.tile(idx.reshape(-1, 16).T, (8, 1)).astype(np.uint16)


def unstriped(offs):
    return offs[:16].T.reshape(-1).astype(np.int64)


def pack_weight(w):
    k, n = w.shape
    w = f64(np.asarray(w, np.float32).astype(ml_dtypes.bfloat16)).reshape(k // 32, 32, n)
    amax = np.abs(w).max(1)
    byte = np.clip(np.where(amax > 0, np.frexp(amax)[1] - 1 + 127 - 7, 1), 1, 254)
    scaled = (w * np.exp2(127.0 - byte)[:, None, :]).reshape(k, n).astype(np.float32)
    words = np.ascontiguousarray(scaled.reshape(k // 512, 128, 4, n).transpose(0, 1, 3, 2)).astype(ml_dtypes.float8_e4m3fn).view(np.uint8)
    return words, np.ascontiguousarray(byte.astype(np.uint8).reshape(k // 512, 16, n))


def unpack_weight(words, scales):
    g, p, n, _ = words.shape
    vals = np.ascontiguousarray(words).view(ml_dtypes.float8_e4m3fn).astype(np.float64) * np.repeat(np.exp2(scales.astype(np.float64) - 127.0), 8, axis=1)[..., None]
    return vals.transpose(0, 1, 3, 2).reshape(g * 512, n)


K, T, S, N = 512, 2048, 1024, 256


def setup_inputs():
    n = np.random.standard_normal
    s = mx_kscale(K)[:, None]
    packed_w1 = pack_weight(n((K, N)) / np.sqrt(3 * K) / s)
    packed_w2 = pack_weight(n((K, N)) / np.sqrt(3 * K) / s)
    packed_w3 = pack_weight(n((K, N)) / np.sqrt(3 * K) / s)
    return {
        "xT": (n((K, T)) * s).astype(np.float32),
        "w1_words": packed_w1[0],
        "w1_scales": packed_w1[1],
        "w2_words": packed_w2[0],
        "w2_scales": packed_w2[1],
        "w3_words": packed_w3[0],
        "w3_scales": packed_w3[1],
        "offs": striped(np.random.permutation(T)[:S]),
    }


def reference(xT, w1_words, w1_scales, w2_words, w2_scales, w3_words, w3_scales, offs):
    xq = mxq(f64(xT)[:, unstriped(offs)], 0, "e4m3")
    y0 = unpack_weight(w1_words, w1_scales).T @ xq
    y1 = unpack_weight(w2_words, w2_scales).T @ xq
    y2 = unpack_weight(w3_words, w3_scales).T @ xq
    return y0 + np.pad(y1, ((0, 0), (1, 0)))[:, :S] + np.pad(y2, ((0, 0), (2, 0)))[:, :S]

@@ -1,0 +1,160 @@
+from contextlib import ExitStack
+
+import concourse.mybir as mybir
+
+K, T, S, N = 512, 2048, 1024, 256
+TAPS = 3
+FLOPS = 2 * TAPS * K * N * S
+
+F32 = mybir.dt.float32
+BF16 = mybir.dt.bfloat16
+I32 = mybir.dt.int32
+U32 = mybir.dt.uint32
+U16 = mybir.dt.uint16
+U8 = mybir.dt.uint8
+FP8X4 = mybir.dt.float8_e4m3fn_x4
+
+P = 128
+PACK = 4
+PHASES = 4
+RUN = 64
+CHUNK = PHASES * RUN
+HALO = TAPS - 1
+CHUNKS = S // CHUNK
+M_TILES = N // P
+
+LOADS = (
+    ((1024, 1024), (512, 384), (512, 384)),
+    ((512, 0), (512, 0), (512, 256), (256, 256), (256, 192)),
+)
+
+
+def tile_picked_listconv_none_e_kernel(
+    tc, xT, w1_words, w1_scales, w2_words, w2_scales, w3_words, w3_scales, offs, out
+):
+    nc = tc.nc
+    with ExitStack() as ctx:
+        keep = ctx.enter_context(tc.tile_pool(name="keep", bufs=1))
+        psum = ctx.enter_context(tc.psum_pool(name="psum", bufs=1))
+
+        offsets = keep.tile([P, S // 16], U16, name="offsets")
+        x_rows = xT.rearrange("(p j) t -> p j t", j=PACK)
+        pairs = [keep.tile([P, 2 * T], BF16, name=f"pairs{h}", align_bytes=64) for h in range(2)]
+
+        def load_half(h):
+            raws = []
+            t0 = 0
+            for i, (width, on_vector) in enumerate(LOADS[h]):
+                raw = keep.tile([P, 2, width], F32, name=f"raw{h}_{i}", align_bytes=64)
+                nc.sync.dma_start(out=raw[:], in_=x_rows[:, 2 * h : 2 * h + 2, t0 : t0 + width])
+                raws.append((raw, t0, width, on_vector))
+                t0 = t0 + width
+            return raws
+
+        def cast_half(h, raws):
+            for raw, t0, width, on_vector in raws:
+                for engine_copy, a, b in (
+                    (nc.vector.tensor_copy, 0, on_vector),
+                    (nc.scalar.copy, on_vector, width),
+                ):
+                    if b > a:
+                        engine_copy(
+                            out=pairs[h][:, 2 * (t0 + a) : 2 * (t0 + b)].rearrange("p (t e) -> p t e", e=2),
+                            in_=raw[:, :, a:b].rearrange("p e t -> p t e"),
+                        )
+
+        raws0 = load_half(0)
+        nc.sync.dma_start(offsets[:], offs)
+        raws1 = load_half(1)
+
+        w_codes, w_scales = [], []
+        for d, (words, scales) in enumerate(
+            ((w1_words, w1_scales), (w2_words, w2_scales), (w3_words, w3_scales))
+        ):
+            codes = keep.tile([P, N], I32, name=f"w_codes{d}", align_bytes=64)
+            nc.sync.dma_start(out=codes[:], in_=words[0].rearrange("p n t -> p (n t)").bitcast(I32))
+            plane = keep.tile([P, N], U8, name=f"w_scales{d}", align_bytes=64)
+            rows = scales[0].bitcast(I32)
+            nc.gpsimd.dma_start(
+                out=plane[0:98, :].bitcast(I32), in_=rows[0:14, :].unsqueeze(0).to_broadcast([7, 14, N // 4])
+            )
+            nc.gpsimd.dma_start(
+                out=plane[98:P, :].bitcast(I32), in_=rows[14:16, :].unsqueeze(0).to_broadcast([15, 2, N // 4])
+            )
+            w_codes.append(codes)
+            w_scales.append(plane)
+
+        picked_all = keep.tile([P, CHUNKS, 2 * CHUNK], I32, name="picked", align_bytes=64)
+        picked = [picked_all[:, c, :] for c in range(CHUNKS)]
+        halo = [keep.tile([P, 2 * HALO * RUN], I32, name=f"halo{c}", align_bytes=64) for c in range(CHUNKS)]
+        x_codes = [keep.tile([P, (HALO + PHASES) * RUN], U32, name=f"x_codes{c}", align_bytes=64) for c in range(CHUNKS)]
+        x_scales = [keep.tile([P, (HALO + PHASES) * RUN], U8, name=f"x_scales{c}", align_bytes=64) for c in range(CHUNKS)]
+
+        nc.vector.memset(halo[0][:].rearrange("p (s w) -> p s w", s=HALO)[:, :, 0:2], 0)
+
+        def gather(h, c):
+            dst = picked[c].bitcast(U32).rearrange("p (r i h) -> p i r h", r=PHASES, h=2)[:, :, :, h]
+            window = pairs[h][:].bitcast(U32)
+            nc.vector.tensor_copy(out=dst, in_=window.indirect(offsets[:, 16 * c : 16 * (c + 1)]))
+
+        def fill_halo(c):
+            late = picked[c].bitcast(U32).rearrange("p (r w) -> p r w", r=PHASES)[:, PHASES - HALO :, :]
+            own = halo[c][:].bitcast(U32).rearrange("p (s w) -> p s w", s=HALO)
+            nc.scalar.copy(out=own[:, :, 2:], in_=late[:, :, : 2 * RUN - 2])
+            if c + 1 < CHUNKS:
+                nxt = halo[c + 1][:].bitcast(U32).rearrange("p (s w) -> p s w", s=HALO)
+                nc.scalar.copy(out=nxt[:, :, 0:2], in_=late[:, :, 2 * RUN - 2 :])
+
+        def quantize(c, src, a, b):
+            nc.vector.quantize_mx(
+                out=x_codes[c][:, a:b].bitcast(FP8X4), scales=x_scales[c][:, a:b], in_=src.bitcast(BF16)
+            )
+
+        cast_half(0, raws0)
+        for c in range(CHUNKS):
+            gather(0, c)
+        cast_half(1, raws1)
+
+        out_rows = out.rearrange("(m p) s -> p m s", p=P)
+        accs = [
+            [psum.tile([P, CHUNK], F32, name=f"acc{c}_{m}") for m in range(M_TILES)] for c in range(CHUNKS)
+        ]
+
+        def tap(c, d, m):
+            cols = slice((HALO - d) * RUN, (HALO - d) * RUN + CHUNK)
+            m_cols = slice(m * P, (m + 1) * P)
+            nc.tensor.matmul_mx(
+                out=accs[c][m][:],
+                lhsT=w_codes[d][:, m_cols].bitcast(FP8X4),
+                lhsT_scale=w_scales[d][:, m_cols],
+                rhs=x_codes[c][:, cols].bitcast(FP8X4),
+                rhs_scale=x_scales[c][:, cols],
+                start=(d == 0),
+                stop=(d == TAPS - 1),
+            )
+
+        def open_chunk(c):
+            quantize(c, picked[c], HALO * RUN, (HALO + PHASES) * RUN)
+            for m in range(M_TILES):
+                tap(c, 0, m)
+
+        def close_chunk(c):
+            quantize(c, halo[c][:], 0, HALO * RUN)
+            for m in range(M_TILES):
+                for d in range(1, TAPS):
+                    tap(c, d, m)
+                result = keep.tile([P, CHUNK], F32, name=f"result{c}_{m}", align_bytes=64)
+                leave = nc.vector.tensor_copy if (c == CHUNKS - 1 and m == M_TILES - 1) else nc.scalar.copy
+                leave(
+                    out=result[:].rearrange("p (i r) -> p i r", r=PHASES),
+                    in_=accs[c][m][:].rearrange("p (r i) -> p i r", r=PHASES),
+                )
+                nc.sync.dma_start(out=out_rows[:, m, c * CHUNK : (c + 1) * CHUNK], in_=result[:])
+
+        for c in range(CHUNKS):
+            gather(1, c)
+            fill_halo(c)
+            if c > 0:
+                close_chunk(c - 1)
+            open_chunk(c)
+        close_chunk(CHUNKS - 1)

@@ -24,9 +24,12 @@ CHUNKS = S // CHUNK
 M_TILES = N // P
 
 LOADS = (
-    ((1024, 1024), (512, 384), (512, 384)),
-    ((512, 0), (512, 0), (512, 256), (256, 256), (256, 192)),
+    ((1024, 1024), (1024, 704)),
+    ((1024, 448), (512, 352), (256, 176), (256, 176)),
 )
+PAD = 4
+HALF = S // 2
+WARMUP = 6
 
 
 def tile_picked_listconv_none_e_kernel(
@@ -84,26 +87,40 @@ def tile_picked_listconv_none_e_kernel(
             w_codes.append(codes)
             w_scales.append(plane)
 
-        picked_all = keep.tile([P, CHUNKS, 2 * CHUNK], I32, name="picked", align_bytes=64)
-        picked = [picked_all[:, c, :] for c in range(CHUNKS)]
+        listed = keep.tile([P, 3, PAD + S // 2], I32, name="listed", align_bytes=64)
+        body = [keep.tile([P, 2 * CHUNK], I32, name=f"body{c}", align_bytes=64) for c in range(CHUNKS)]
         halo = [keep.tile([P, 2 * HALO * RUN], I32, name=f"halo{c}", align_bytes=64) for c in range(CHUNKS)]
         x_codes = [keep.tile([P, (HALO + PHASES) * RUN], U32, name=f"x_codes{c}", align_bytes=64) for c in range(CHUNKS)]
         x_scales = [keep.tile([P, (HALO + PHASES) * RUN], U8, name=f"x_scales{c}", align_bytes=64) for c in range(CHUNKS)]
 
-        nc.vector.memset(halo[0][:].rearrange("p (s w) -> p s w", s=HALO)[:, :, 0:2], 0)
+        nc.vector.memset(listed[:, 0::2, 0:PAD], 0)
 
-        def gather(h, c):
-            dst = picked[c].bitcast(U32).rearrange("p (r i h) -> p i r h", r=PHASES, h=2)[:, :, :, h]
+        def gather(h, j0, count):
+            row = 2 if h == 1 else j0 // HALF
+            col = PAD + j0 % HALF
             window = pairs[h][:].bitcast(U32)
-            nc.vector.tensor_copy(out=dst, in_=window.indirect(offsets[:, 16 * c : 16 * (c + 1)]))
+            nc.vector.tensor_copy(
+                out=listed[:, row, col : col + count].bitcast(U32),
+                in_=window.indirect(offsets[:, j0 // 16 : (j0 + count) // 16]),
+            )
 
-        def fill_halo(c):
-            late = picked[c].bitcast(U32).rearrange("p (r w) -> p r w", r=PHASES)[:, PHASES - HALO :, :]
-            own = halo[c][:].bitcast(U32).rearrange("p (s w) -> p s w", s=HALO)
-            nc.scalar.copy(out=own[:, :, 2:], in_=late[:, :, : 2 * RUN - 2])
-            if c + 1 < CHUNKS:
-                nxt = halo[c + 1][:].bitcast(U32).rearrange("p (s w) -> p s w", s=HALO)
-                nc.scalar.copy(out=nxt[:, :, 0:2], in_=late[:, :, 2 * RUN - 2 :])
+        def entries(c, back, dtype):
+            row = c * CHUNK // HALF
+            col = PAD + c * CHUNK % HALF - back
+            both = listed[:, row :: 2 - row, col : col + CHUNK].bitcast(dtype)
+            return both.rearrange("p h (i r) -> p i r h", r=PHASES)
+
+        def weave_body(c):
+            nc.scalar.copy(
+                out=body[c][:].bitcast(U32).rearrange("p (r i h) -> p i r h", r=PHASES, h=2),
+                in_=entries(c, 0, U32),
+            )
+
+        def weave_halo(c):
+            nc.vector.tensor_copy(
+                out=halo[c][:].rearrange("p (s i h) -> p i s h", s=HALO, h=2),
+                in_=entries(c, PHASES, I32)[:, :, PHASES - HALO :, :],
+            )
 
         def quantize(c, src, a, b):
             nc.vector.quantize_mx(
@@ -111,8 +128,8 @@ def tile_picked_listconv_none_e_kernel(
             )
 
         cast_half(0, raws0)
-        for c in range(CHUNKS):
-            gather(0, c)
+        gather(0, 0, HALF)
+        gather(0, HALF, HALF)
         cast_half(1, raws1)
 
         out_rows = out.rearrange("(m p) s -> p m s", p=P)
@@ -133,15 +150,22 @@ def tile_picked_listconv_none_e_kernel(
                 stop=(d == TAPS - 1),
             )
 
-        def open_chunk(c):
-            quantize(c, picked[c], HALO * RUN, (HALO + PHASES) * RUN)
-            for m in range(M_TILES):
-                tap(c, 0, m)
+        for i in range(WARMUP):
+            nc.tensor.matmul_mx(
+                out=accs[CHUNKS - 1][M_TILES - 1][:],
+                lhsT=w_codes[1][:, 0:P].bitcast(FP8X4),
+                lhsT_scale=w_scales[1][:, 0:P],
+                rhs=w_codes[1][:].bitcast(FP8X4),
+                rhs_scale=w_scales[1][:],
+                start=True,
+                stop=True,
+            )
 
-        def close_chunk(c):
+        def multiply(c):
+            quantize(c, body[c][:], HALO * RUN, (HALO + PHASES) * RUN)
             quantize(c, halo[c][:], 0, HALO * RUN)
             for m in range(M_TILES):
-                for d in range(1, TAPS):
+                for d in range(TAPS):
                     tap(c, d, m)
                 result = keep.tile([P, CHUNK], F32, name=f"result{c}_{m}", align_bytes=64)
                 leave = nc.vector.tensor_copy if (c == CHUNKS - 1 and m == M_TILES - 1) else nc.scalar.copy
@@ -152,9 +176,13 @@ def tile_picked_listconv_none_e_kernel(
                 nc.sync.dma_start(out=out_rows[:, m, c * CHUNK : (c + 1) * CHUNK], in_=result[:])
 
         for c in range(CHUNKS):
-            gather(1, c)
-            fill_halo(c)
+            gather(1, c * CHUNK, CHUNK)
+            weave_body(c)
+            if c == 1:
+                weave_halo(0)
             if c > 0:
-                close_chunk(c - 1)
-            open_chunk(c)
-        close_chunk(CHUNKS - 1)
+                multiply(c - 1)
+                weave_halo(c)
+            if (c + 1) * CHUNK == HALF:
+                nc.vector.tensor_copy(out=listed[:, 1:3, 0:PAD], in_=listed[:, 0::2, HALF : HALF + PAD])
+        multiply(CHUNKS - 1)

@@ -78,7 +78,7 @@ def tile_picked_listconv_none_e_kernel(
             nc.sync.dma_start(out=codes[:], in_=words[0].rearrange("p n t -> p (n t)").bitcast(I32))
             plane = keep.tile([P, N], U8, name=f"w_scales{d}", align_bytes=64)
             rows = scales[0].bitcast(I32)
-            nc.gpsimd.dma_start(
+            nc.sync.dma_start(
                 out=plane[0:98, :].bitcast(I32), in_=rows[0:14, :].unsqueeze(0).to_broadcast([7, 14, N // 4])
             )
             nc.gpsimd.dma_start(
@@ -146,17 +146,17 @@ def tile_picked_listconv_none_e_kernel(
                 lhsT_scale=w_scales[d][:, m_cols],
                 rhs=x_codes[c][:, cols].bitcast(FP8X4),
                 rhs_scale=x_scales[c][:, cols],
-                start=(d == 0),
-                stop=(d == TAPS - 1),
+                start=(d == TAPS - 1),
+                stop=(d == 0),
             )
 
         for i in range(WARMUP):
             nc.tensor.matmul_mx(
                 out=accs[CHUNKS - 1][M_TILES - 1][:],
-                lhsT=w_codes[1][:, 0:P].bitcast(FP8X4),
-                lhsT_scale=w_scales[1][:, 0:P],
-                rhs=w_codes[1][:].bitcast(FP8X4),
-                rhs_scale=w_scales[1][:],
+                lhsT=w_codes[0][:, 0:P].bitcast(FP8X4),
+                lhsT_scale=w_scales[0][:, 0:P],
+                rhs=w_codes[0][:].bitcast(FP8X4),
+                rhs_scale=w_scales[0][:],
                 start=True,
                 stop=True,
             )
@@ -165,7 +165,7 @@ def tile_picked_listconv_none_e_kernel(
             quantize(c, body[c][:], HALO * RUN, (HALO + PHASES) * RUN)
             quantize(c, halo[c][:], 0, HALO * RUN)
             for m in range(M_TILES):
-                for d in range(TAPS):
+                for d in reversed(range(TAPS)):
                     tap(c, d, m)
                 result = keep.tile([P, CHUNK], F32, name=f"result{c}_{m}", align_bytes=64)
                 leave = nc.vector.tensor_copy if (c == CHUNKS - 1 and m == M_TILES - 1) else nc.scalar.copy

@@ -24,8 +24,8 @@ CHUNKS = S // CHUNK
 M_TILES = N // P
 
 LOADS = (
-    ((1024, 1024), (1024, 704)),
-    ((1024, 448), (512, 352), (256, 176), (256, 176)),
+    ((1024, 1024), (512, 512), (512, 352)),
+    ((1024, 352), (512, 352), (256, 176), (256, 176)),
 )
 PAD = 4
 HALF = S // 2
@@ -88,9 +88,12 @@ def tile_picked_listconv_none_e_kernel(
             w_scales.append(plane)
 
         listed = keep.tile([P, 3, PAD + S // 2], I32, name="listed", align_bytes=64)
-        body = [keep.tile([P, 2 * CHUNK], I32, name=f"body{c}", align_bytes=64) for c in range(CHUNKS)]
         halo = [keep.tile([P, 2 * HALO * RUN], I32, name=f"halo{c}", align_bytes=64) for c in range(CHUNKS)]
-        x_codes = [keep.tile([P, (HALO + PHASES) * RUN], U32, name=f"x_codes{c}", align_bytes=64) for c in range(CHUNKS)]
+        x_codes = [
+            keep.tile([P, (HALO + PHASES) * RUN], U32, name=f"x_codes{c}", tag=f"slot{c}", align_bytes=64)
+            for c in range(CHUNKS)
+        ]
+        body = []
         x_scales = [keep.tile([P, (HALO + PHASES) * RUN], U8, name=f"x_scales{c}", align_bytes=64) for c in range(CHUNKS)]
 
         nc.vector.memset(listed[:, 0::2, 0:PAD], 0)
@@ -111,6 +114,8 @@ def tile_picked_listconv_none_e_kernel(
             return both.rearrange("p h (i r) -> p i r h", r=PHASES)
 
         def weave_body(c):
+            tag = "slot0" if c == CHUNKS - 1 else f"body{c}"
+            body.append(keep.tile([P, 2 * CHUNK], I32, name=f"body{c}", tag=tag, align_bytes=64))
             nc.scalar.copy(
                 out=body[c][:].bitcast(U32).rearrange("p (r i h) -> p i r h", r=PHASES, h=2),
                 in_=entries(c, 0, U32),
@@ -167,8 +172,11 @@ def tile_picked_listconv_none_e_kernel(
             for m in range(M_TILES):
                 for d in reversed(range(TAPS)):
                     tap(c, d, m)
+
+        def store(c):
+            for m in range(M_TILES):
                 result = keep.tile([P, CHUNK], F32, name=f"result{c}_{m}", align_bytes=64)
-                leave = nc.vector.tensor_copy if (c == CHUNKS - 1 and m == M_TILES - 1) else nc.scalar.copy
+                leave = nc.vector.tensor_copy if (c >= CHUNKS - 2 and m == M_TILES - 1) else nc.scalar.copy
                 leave(
                     out=result[:].rearrange("p (i r) -> p i r", r=PHASES),
                     in_=accs[c][m][:].rearrange("p (r i) -> p i r", r=PHASES),
@@ -178,6 +186,8 @@ def tile_picked_listconv_none_e_kernel(
         for c in range(CHUNKS):
             gather(1, c * CHUNK, CHUNK)
             weave_body(c)
+            if c > 1:
+                store(c - 2)
             if c == 1:
                 weave_halo(0)
             if c > 0:
@@ -186,3 +196,5 @@ def tile_picked_listconv_none_e_kernel(
             if (c + 1) * CHUNK == HALF:
                 nc.vector.tensor_copy(out=listed[:, 1:3, 0:PAD], in_=listed[:, 0::2, HALF : HALF + PAD])
         multiply(CHUNKS - 1)
+        store(CHUNKS - 2)
+        store(CHUNKS - 1)

@@ -27,7 +27,8 @@ LOADS = (
     ((1024, 1024), (512, 512), (512, 352)),
     ((1024, 352), (512, 352), (256, 176), (256, 176)),
 )
-PAD = 4
+PAD = 16
+ROW = PAD + S + CHUNK
 HALF = S // 2
 WARMUP = 6
 
@@ -70,10 +71,10 @@ def tile_picked_listconv_none_e_kernel(
         nc.sync.dma_start(offsets[:], offs)
         raws1 = load_half(1)
 
-        w_codes, w_scales = [], []
-        for d, (words, scales) in enumerate(
-            ((w1_words, w1_scales), (w2_words, w2_scales), (w3_words, w3_scales))
-        ):
+        w_codes, w_scales = {}, {}
+        weights = ((w1_words, w1_scales), (w2_words, w2_scales), (w3_words, w3_scales))
+        for d in reversed(range(TAPS)):
+            words, scales = weights[d]
             codes = keep.tile([P, N], I32, name=f"w_codes{d}", align_bytes=64)
             nc.sync.dma_start(out=codes[:], in_=words[0].rearrange("p n t -> p (n t)").bitcast(I32))
             plane = keep.tile([P, N], U8, name=f"w_scales{d}", align_bytes=64)
@@ -84,11 +85,12 @@ def tile_picked_listconv_none_e_kernel(
             nc.gpsimd.dma_start(
                 out=plane[98:P, :].bitcast(I32), in_=rows[14:16, :].unsqueeze(0).to_broadcast([15, 2, N // 4])
             )
-            w_codes.append(codes)
-            w_scales.append(plane)
+            w_codes[d] = codes
+            w_scales[d] = plane
 
-        listed = keep.tile([P, 3, PAD + S // 2], I32, name="listed", align_bytes=64)
-        halo = [keep.tile([P, 2 * HALO * RUN], I32, name=f"halo{c}", align_bytes=64) for c in range(CHUNKS)]
+        listed = keep.tile([P, 2 * ROW], I32, name="listed", align_bytes=64)
+        listed_rows = listed[:].rearrange("p (h x) -> p h x", h=2)
+        halo = []
         x_codes = [
             keep.tile([P, (HALO + PHASES) * RUN], U32, name=f"x_codes{c}", tag=f"slot{c}", align_bytes=64)
             for c in range(CHUNKS)
@@ -96,35 +98,39 @@ def tile_picked_listconv_none_e_kernel(
         body = []
         x_scales = [keep.tile([P, (HALO + PHASES) * RUN], U8, name=f"x_scales{c}", align_bytes=64) for c in range(CHUNKS)]
 
-        nc.vector.memset(listed[:, 0::2, 0:PAD], 0)
+        nc.vector.memset(listed_rows[:, :, PAD - 4 : PAD], 0)
 
         def gather(h, j0, count):
-            row = 2 if h == 1 else j0 // HALF
-            col = PAD + j0 % HALF
+            col = h * ROW + PAD + j0
             window = pairs[h][:].bitcast(U32)
             nc.vector.tensor_copy(
-                out=listed[:, row, col : col + count].bitcast(U32),
+                out=listed[:, col : col + count].bitcast(U32),
                 in_=window.indirect(offsets[:, j0 // 16 : (j0 + count) // 16]),
             )
 
-        def entries(c, back, dtype):
-            row = c * CHUNK // HALF
-            col = PAD + c * CHUNK % HALF - back
-            both = listed[:, row :: 2 - row, col : col + CHUNK].bitcast(dtype)
+        def entries(c, back):
+            col = PAD + c * CHUNK - back
+            both = listed_rows[:, :, col : col + CHUNK].bitcast(U32)
             return both.rearrange("p h (i r) -> p i r h", r=PHASES)
 
         def weave_body(c):
-            tag = "slot0" if c == CHUNKS - 1 else f"body{c}"
-            body.append(keep.tile([P, 2 * CHUNK], I32, name=f"body{c}", tag=tag, align_bytes=64))
+            if c == 0:
+                col = ROW + PAD + (CHUNKS - 1) * CHUNK
+                body.append(listed[:, col : col + 2 * CHUNK])
+            else:
+                woven = keep.tile([P, 2 * CHUNK], I32, name=f"body{c}", align_bytes=64)
+                body.append(woven[:])
             nc.scalar.copy(
-                out=body[c][:].bitcast(U32).rearrange("p (r i h) -> p i r h", r=PHASES, h=2),
-                in_=entries(c, 0, U32),
+                out=body[c].bitcast(U32).rearrange("p (r i h) -> p i r h", r=PHASES, h=2),
+                in_=entries(c, 0),
             )
 
         def weave_halo(c):
-            nc.vector.tensor_copy(
-                out=halo[c][:].rearrange("p (s i h) -> p i s h", s=HALO, h=2),
-                in_=entries(c, PHASES, I32)[:, :, PHASES - HALO :, :],
+            tag = "slot0" if c == CHUNKS - 1 else f"halo{c}"
+            halo.append(keep.tile([P, 2 * HALO * RUN], I32, name=f"halo{c}", tag=tag, align_bytes=64))
+            nc.scalar.copy(
+                out=halo[c][:].bitcast(U32).rearrange("p (s i h) -> p i s h", s=HALO, h=2),
+                in_=entries(c, HALO)[:, :, 0:HALO, :],
             )
 
         def quantize(c, src, a, b):
@@ -151,50 +157,52 @@ def tile_picked_listconv_none_e_kernel(
                 lhsT_scale=w_scales[d][:, m_cols],
                 rhs=x_codes[c][:, cols].bitcast(FP8X4),
                 rhs_scale=x_scales[c][:, cols],
-                start=(d == TAPS - 1),
-                stop=(d == 0),
+                start=(d == 0),
+                stop=(d == TAPS - 1),
             )
 
         for i in range(WARMUP):
             nc.tensor.matmul_mx(
                 out=accs[CHUNKS - 1][M_TILES - 1][:],
-                lhsT=w_codes[0][:, 0:P].bitcast(FP8X4),
-                lhsT_scale=w_scales[0][:, 0:P],
-                rhs=w_codes[0][:].bitcast(FP8X4),
-                rhs_scale=w_scales[0][:],
+                lhsT=w_codes[TAPS - 1][:, 0:P].bitcast(FP8X4),
+                lhsT_scale=w_scales[TAPS - 1][:, 0:P],
+                rhs=w_codes[TAPS - 1][:].bitcast(FP8X4),
+                rhs_scale=w_scales[TAPS - 1][:],
                 start=True,
                 stop=True,
             )
 
         def multiply(c):
-            quantize(c, body[c][:], HALO * RUN, (HALO + PHASES) * RUN)
+            quantize(c, body[c], HALO * RUN, (HALO + PHASES) * RUN)
             quantize(c, halo[c][:], 0, HALO * RUN)
             for m in range(M_TILES):
-                for d in reversed(range(TAPS)):
+                tap(c, 0, m)
+            for m in range(M_TILES):
+                for d in range(1, TAPS):
                     tap(c, d, m)
 
-        def store(c):
-            for m in range(M_TILES):
-                result = keep.tile([P, CHUNK], F32, name=f"result{c}_{m}", align_bytes=64)
-                leave = nc.vector.tensor_copy if (c >= CHUNKS - 2 and m == M_TILES - 1) else nc.scalar.copy
-                leave(
-                    out=result[:].rearrange("p (i r) -> p i r", r=PHASES),
-                    in_=accs[c][m][:].rearrange("p (r i) -> p i r", r=PHASES),
-                )
-                nc.sync.dma_start(out=out_rows[:, m, c * CHUNK : (c + 1) * CHUNK], in_=result[:])
+        def store(c, m):
+            result = keep.tile([P, CHUNK], F32, name=f"result{c}_{m}", align_bytes=64)
+            leave = nc.vector.tensor_copy if m == M_TILES - 1 else nc.scalar.copy
+            leave(
+                out=result[:].rearrange("p (i r) -> p i r", r=PHASES),
+                in_=accs[c][m][:].rearrange("p (r i) -> p i r", r=PHASES),
+            )
+            nc.sync.dma_start(out=out_rows[:, m, c * CHUNK : (c + 1) * CHUNK], in_=result[:])
 
-        for c in range(CHUNKS):
+        for c in range(CHUNKS - 1):
             gather(1, c * CHUNK, CHUNK)
             weave_body(c)
-            if c > 1:
-                store(c - 2)
-            if c == 1:
-                weave_halo(0)
-            if c > 0:
-                multiply(c - 1)
-                weave_halo(c)
-            if (c + 1) * CHUNK == HALF:
-                nc.vector.tensor_copy(out=listed[:, 1:3, 0:PAD], in_=listed[:, 0::2, HALF : HALF + PAD])
-        multiply(CHUNKS - 1)
-        store(CHUNKS - 2)
-        store(CHUNKS - 1)
+            weave_halo(c)
+        multiply(0)
+        gather(1, (CHUNKS - 1) * CHUNK, CHUNK)
+        multiply(1)
+        weave_body(CHUNKS - 1)
+        store(0, 0)
+        weave_halo(CHUNKS - 1)
+        multiply(2)
+        store(0, 1)
+        multiply(3)
+        for c in range(1, CHUNKS):
+            for m in range(M_TILES):
+                store(c, m)

@@ -23,9 +23,14 @@ HALO = TAPS - 1
 CHUNKS = S // CHUNK
 M_TILES = N // P
 
+HALF_T = T // 2
 LOADS = (
-    ((1024, 1024), (512, 512), (512, 352)),
-    ((1024, 352), (512, 352), (256, 176), (256, 176)),
+    ((0, 2, 0, 1024), (0, 2, 1024, 2048)),
+    ((0, 2, 0, 1024), (0, 1, 1024, 2048), (1, 2, 1024, 1536), (1, 2, 1536, 1792), (1, 2, 1792, 2048)),
+)
+CASTS = (
+    ((0, 688, 1024), (1024, 1712, 2048)),
+    ((0, 352, 1024), (1024, 1376, 1536), (1536, 1712, 1792), (1792, 1968, 2048)),
 )
 PAD = 16
 ROW = PAD + S + CHUNK
@@ -46,26 +51,23 @@ def tile_picked_listconv_none_e_kernel(
         pairs = [keep.tile([P, 2 * T], BF16, name=f"pairs{h}", align_bytes=64) for h in range(2)]
 
         def load_half(h):
-            raws = []
-            t0 = 0
-            for i, (width, on_vector) in enumerate(LOADS[h]):
-                raw = keep.tile([P, 2, width], F32, name=f"raw{h}_{i}", align_bytes=64)
-                nc.sync.dma_start(out=raw[:], in_=x_rows[:, 2 * h : 2 * h + 2, t0 : t0 + width])
-                raws.append((raw, t0, width, on_vector))
-                t0 = t0 + width
-            return raws
+            raw = [keep.tile([P, 2, HALF_T], F32, name=f"raw{h}_{i}", align_bytes=64) for i in range(2)]
+            for e0, e1, t0, t1 in LOADS[h]:
+                i = t0 // HALF_T
+                nc.sync.dma_start(
+                    out=raw[i][:, e0:e1, t0 - i * HALF_T : t1 - i * HALF_T],
+                    in_=x_rows[:, 2 * h + e0 : 2 * h + e1, t0:t1],
+                )
+            return raw
 
-        def cast_half(h, raws):
-            for raw, t0, width, on_vector in raws:
-                for engine_copy, a, b in (
-                    (nc.vector.tensor_copy, 0, on_vector),
-                    (nc.scalar.copy, on_vector, width),
-                ):
-                    if b > a:
-                        engine_copy(
-                            out=pairs[h][:, 2 * (t0 + a) : 2 * (t0 + b)].rearrange("p (t e) -> p t e", e=2),
-                            in_=raw[:, :, a:b].rearrange("p e t -> p t e"),
-                        )
+        def cast_half(h, raw):
+            for t0, split, t1 in CASTS[h]:
+                i = t0 // HALF_T
+                for engine_copy, a, b in ((nc.vector.tensor_copy, t0, split), (nc.scalar.copy, split, t1)):
+                    engine_copy(
+                        out=pairs[h][:, 2 * a : 2 * b].rearrange("p (t e) -> p t e", e=2),
+                        in_=raw[i][:, :, a - i * HALF_T : b - i * HALF_T].rearrange("p e t -> p t e"),
+                    )
 
         raws0 = load_half(0)
         nc.sync.dma_start(offsets[:], offs)

@@ -25,17 +25,18 @@ M_TILES = N // P
 
 HALF_T = T // 2
 LOADS = (
-    ((0, 2, 0, 1024), (0, 2, 1024, 2048)),
+    ((0, 2, 0, 1024), (0, 1, 1024, 2048), (1, 2, 1024, 1536), (1, 2, 1536, 2048)),
     ((0, 2, 0, 1024), (0, 1, 1024, 2048), (1, 2, 1024, 1536), (1, 2, 1536, 1792), (1, 2, 1792, 2048)),
 )
 CASTS = (
-    ((0, 688, 1024), (1024, 1712, 2048)),
+    ((0, 688, 1024), (1024, 1376, 1536), (1536, 1888, 2048)),
     ((0, 352, 1024), (1024, 1376, 1536), (1536, 1712, 1792), (1792, 1968, 2048)),
 )
 PAD = 16
 ROW = PAD + S + CHUNK
 HALF = S // 2
-WARMUP = 6
+WARMUP = 3
+WARMUP_N = 512
 
 
 def tile_picked_listconv_none_e_kernel(
@@ -77,15 +78,19 @@ def tile_picked_listconv_none_e_kernel(
         weights = ((w1_words, w1_scales), (w2_words, w2_scales), (w3_words, w3_scales))
         for d in reversed(range(TAPS)):
             words, scales = weights[d]
-            codes = keep.tile([P, N], I32, name=f"w_codes{d}", align_bytes=64)
-            nc.sync.dma_start(out=codes[:], in_=words[0].rearrange("p n t -> p (n t)").bitcast(I32))
-            plane = keep.tile([P, N], U8, name=f"w_scales{d}", align_bytes=64)
+            width = WARMUP_N if d == TAPS - 1 else N
+            codes = keep.tile([P, width], I32, name=f"w_codes{d}", align_bytes=64)
+            plane = keep.tile([P, width], U8, name=f"w_scales{d}", align_bytes=64)
+            if width > N:
+                nc.vector.memset(codes[:, N:width], 0)
+                nc.vector.memset(plane[:, N:width].bitcast(I32), 0)
+            nc.sync.dma_start(out=codes[:, 0:N], in_=words[0].rearrange("p n t -> p (n t)").bitcast(I32))
             rows = scales[0].bitcast(I32)
             nc.sync.dma_start(
-                out=plane[0:98, :].bitcast(I32), in_=rows[0:14, :].unsqueeze(0).to_broadcast([7, 14, N // 4])
+                out=plane[0:98, 0:N].bitcast(I32), in_=rows[0:14, :].unsqueeze(0).to_broadcast([7, 14, N // 4])
             )
             nc.gpsimd.dma_start(
-                out=plane[98:P, :].bitcast(I32), in_=rows[14:16, :].unsqueeze(0).to_broadcast([15, 2, N // 4])
+                out=plane[98:P, 0:N].bitcast(I32), in_=rows[14:16, :].unsqueeze(0).to_broadcast([15, 2, N // 4])
             )
             w_codes[d] = codes
             w_scales[d] = plane
@@ -147,14 +152,14 @@ def tile_picked_listconv_none_e_kernel(
 
         out_rows = out.rearrange("(m p) s -> p m s", p=P)
         accs = [
-            [psum.tile([P, CHUNK], F32, name=f"acc{c}_{m}") for m in range(M_TILES)] for c in range(CHUNKS)
+            [psum.tile([P, WARMUP_N], F32, name=f"acc{c}_{m}") for m in range(M_TILES)] for c in range(CHUNKS)
         ]
 
-        def tap(c, d, m):
-            cols = slice((HALO - d) * RUN, (HALO - d) * RUN + CHUNK)
+        def tap(c, d, m, r0, r1):
+            cols = slice((HALO - d + r0) * RUN, (HALO - d + r1) * RUN)
             m_cols = slice(m * P, (m + 1) * P)
             nc.tensor.matmul_mx(
-                out=accs[c][m][:],
+                out=accs[c][m][:, r0 * RUN : r1 * RUN],
                 lhsT=w_codes[d][:, m_cols].bitcast(FP8X4),
                 lhsT_scale=w_scales[d][:, m_cols],
                 rhs=x_codes[c][:, cols].bitcast(FP8X4),
@@ -177,18 +182,24 @@ def tile_picked_listconv_none_e_kernel(
         def multiply(c):
             quantize(c, body[c], HALO * RUN, (HALO + PHASES) * RUN)
             quantize(c, halo[c][:], 0, HALO * RUN)
+            first = 0
+            if c == 0:
+                for m in range(M_TILES):
+                    for d in range(TAPS):
+                        tap(c, d, m, HALO, PHASES)
+            last = HALO if c == 0 else PHASES
             for m in range(M_TILES):
-                tap(c, 0, m)
+                tap(c, 0, m, first, last)
             for m in range(M_TILES):
                 for d in range(1, TAPS):
-                    tap(c, d, m)
+                    tap(c, d, m, first, last)
 
         def store(c, m):
             result = keep.tile([P, CHUNK], F32, name=f"result{c}_{m}", align_bytes=64)
             leave = nc.vector.tensor_copy if m == M_TILES - 1 else nc.scalar.copy
             leave(
                 out=result[:].rearrange("p (i r) -> p i r", r=PHASES),
-                in_=accs[c][m][:].rearrange("p (r i) -> p i r", r=PHASES),
+                in_=accs[c][m][:, 0:CHUNK].rearrange("p (r i) -> p i r", r=PHASES),
             )
             nc.sync.dma_start(out=out_rows[:, m, c * CHUNK : (c + 1) * CHUNK], in_=result[:])
 

@@ -13,30 +13,30 @@ U32 = mybir.dt.uint32
 U16 = mybir.dt.uint16
 U8 = mybir.dt.uint8
 FP8X4 = mybir.dt.float8_e4m3fn_x4
+ADD = mybir.AluOpType.add
 
 P = 128
 PACK = 4
-PHASES = 4
-RUN = 64
-CHUNK = PHASES * RUN
-HALO = TAPS - 1
+LANES = 16
+PHASES = 16
+CHUNK = LANES * PHASES
+OVER = TAPS - 1
 CHUNKS = S // CHUNK
 M_TILES = N // P
+BANK = 512
 
-HALF_T = T // 2
 LOADS = (
     ((0, 2, 0, 1024), (0, 1, 1024, 2048), (1, 2, 1024, 1536), (1, 2, 1536, 2048)),
-    ((0, 2, 0, 1024), (0, 1, 1024, 2048), (1, 2, 1024, 1536), (1, 2, 1536, 1792), (1, 2, 1792, 2048)),
+    ((0, 2, 0, 512), (0, 2, 512, 1024), (0, 1, 1024, 2048), (1, 2, 1024, 1536), (1, 2, 1536, 1792), (1, 2, 1792, 2048)),
 )
 CASTS = (
     ((0, 688, 1024), (1024, 1376, 1536), (1536, 1888, 2048)),
-    ((0, 352, 1024), (1024, 1376, 1536), (1536, 1712, 1792), (1792, 1968, 2048)),
+    ((0, 0, 512), (512, 512, 1024), (1024, 1376, 1536), (1536, 1712, 1792), (1792, 1792, 2048)),
 )
-PAD = 16
-ROW = PAD + S + CHUNK
-HALF = S // 2
-WARMUP = 3
-WARMUP_N = 512
+OPEN_N = (512, 256)
+SHIFTED = 2
+RUN = 64
+RUNS = CHUNK // RUN
 
 
 def tile_picked_listconv_none_e_kernel(
@@ -52,22 +52,17 @@ def tile_picked_listconv_none_e_kernel(
         pairs = [keep.tile([P, 2 * T], BF16, name=f"pairs{h}", align_bytes=64) for h in range(2)]
 
         def load_half(h):
-            raw = [keep.tile([P, 2, HALF_T], F32, name=f"raw{h}_{i}", align_bytes=64) for i in range(2)]
+            raw = keep.tile([P, 2, T], F32, name=f"raw{h}", align_bytes=64)
             for e0, e1, t0, t1 in LOADS[h]:
-                i = t0 // HALF_T
-                nc.sync.dma_start(
-                    out=raw[i][:, e0:e1, t0 - i * HALF_T : t1 - i * HALF_T],
-                    in_=x_rows[:, 2 * h + e0 : 2 * h + e1, t0:t1],
-                )
+                nc.sync.dma_start(out=raw[:, e0:e1, t0:t1], in_=x_rows[:, 2 * h + e0 : 2 * h + e1, t0:t1])
             return raw
 
-        def cast_half(h, raw):
-            for t0, split, t1 in CASTS[h]:
-                i = t0 // HALF_T
-                for engine_copy, a, b in ((nc.vector.tensor_copy, t0, split), (nc.scalar.copy, split, t1)):
+        def cast(h, raw, t0, split, t1):
+            for engine_copy, a, b in ((nc.vector.tensor_copy, t0, split), (nc.scalar.copy, split, t1)):
+                if a < b:
                     engine_copy(
                         out=pairs[h][:, 2 * a : 2 * b].rearrange("p (t e) -> p t e", e=2),
-                        in_=raw[i][:, :, a - i * HALF_T : b - i * HALF_T].rearrange("p e t -> p t e"),
+                        in_=raw[:, :, a:b].rearrange("p e t -> p t e"),
                     )
 
         raws0 = load_half(0)
@@ -78,144 +73,189 @@ def tile_picked_listconv_none_e_kernel(
         weights = ((w1_words, w1_scales), (w2_words, w2_scales), (w3_words, w3_scales))
         for d in reversed(range(TAPS)):
             words, scales = weights[d]
-            width = WARMUP_N if d == TAPS - 1 else N
-            codes = keep.tile([P, width], I32, name=f"w_codes{d}", align_bytes=64)
-            plane = keep.tile([P, width], U8, name=f"w_scales{d}", align_bytes=64)
-            if width > N:
-                nc.vector.memset(codes[:, N:width], 0)
-                nc.vector.memset(plane[:, N:width].bitcast(I32), 0)
-            nc.sync.dma_start(out=codes[:, 0:N], in_=words[0].rearrange("p n t -> p (n t)").bitcast(I32))
+            codes = keep.tile([P, N], I32, name=f"w_codes{d}", align_bytes=64)
+            plane = keep.tile([P, N], U8, name=f"w_scales{d}", align_bytes=64)
+            nc.sync.dma_start(out=codes[:], in_=words[0].rearrange("p n t -> p (n t)").bitcast(I32))
             rows = scales[0].bitcast(I32)
             nc.sync.dma_start(
-                out=plane[0:98, 0:N].bitcast(I32), in_=rows[0:14, :].unsqueeze(0).to_broadcast([7, 14, N // 4])
+                out=plane[0:98, :].bitcast(I32), in_=rows[0:14, :].unsqueeze(0).to_broadcast([7, 14, N // 4])
             )
             nc.gpsimd.dma_start(
-                out=plane[98:P, 0:N].bitcast(I32), in_=rows[14:16, :].unsqueeze(0).to_broadcast([15, 2, N // 4])
+                out=plane[98:P, :].bitcast(I32), in_=rows[14:16, :].unsqueeze(0).to_broadcast([15, 2, N // 4])
             )
             w_codes[d] = codes
             w_scales[d] = plane
 
-        listed = keep.tile([P, 2 * ROW], I32, name="listed", align_bytes=64)
-        listed_rows = listed[:].rearrange("p (h x) -> p h x", h=2)
-        halo = []
+        early = (5 * CHUNK, 0, CHUNK, 2 * CHUNK)
+        late = (6 * CHUNK, 3 * CHUNK, 4 * CHUNK, 5 * CHUNK)
+        listed = keep.tile([P, 8 * CHUNK], I32, name="listed", align_bytes=64)
+        body, halo = {}, {}
+        widths = (CHUNK + BANK, CHUNK, CHUNK + OVER * RUN, CHUNK + OVER * RUN)
         x_codes = [
-            keep.tile([P, (HALO + PHASES) * RUN], U32, name=f"x_codes{c}", tag=f"slot{c}", align_bytes=64)
-            for c in range(CHUNKS)
+            keep.tile([P, widths[c]], I32, name=f"x_codes{c}", tag=f"slot{c}", align_bytes=64) for c in range(CHUNKS)
         ]
-        body = []
-        x_scales = [keep.tile([P, (HALO + PHASES) * RUN], U8, name=f"x_scales{c}", align_bytes=64) for c in range(CHUNKS)]
+        nc.vector.memset(x_codes[0][:, CHUNK:], 0)
+        results = [keep.tile([P, S], F32, name=f"result{m}", align_bytes=64) for m in range(M_TILES)]
+        for m in range(M_TILES):
+            nc.vector.memset(results[m][:, 0:OVER], 0.0)
 
-        nc.vector.memset(listed_rows[:, :, PAD - 4 : PAD], 0)
-
-        def gather(h, j0, count):
-            col = h * ROW + PAD + j0
+        def gather(h, j0, count, col):
             window = pairs[h][:].bitcast(U32)
             nc.vector.tensor_copy(
                 out=listed[:, col : col + count].bitcast(U32),
                 in_=window.indirect(offsets[:, j0 // 16 : (j0 + count) // 16]),
             )
 
-        def entries(c, back):
-            col = PAD + c * CHUNK - back
-            both = listed_rows[:, :, col : col + CHUNK].bitcast(U32)
-            return both.rearrange("p h (i r) -> p i r h", r=PHASES)
+        def gather_plane(e):
+            halves = listed[:, late[0] : late[0] + CHUNK].bitcast(BF16).rearrange("p (j e) -> p j e", e=2)
+            nc.vector.tensor_copy(out=halves[:, :, e], in_=raws1[:, e, :].indirect(offsets[:, 0 : CHUNK // 16]))
 
-        def weave_body(c):
+        def gather_late(c):
             if c == 0:
-                col = ROW + PAD + (CHUNKS - 1) * CHUNK
-                body.append(listed[:, col : col + 2 * CHUNK])
+                gather_plane(1)
             else:
-                woven = keep.tile([P, 2 * CHUNK], I32, name=f"body{c}", align_bytes=64)
-                body.append(woven[:])
-            nc.scalar.copy(
-                out=body[c].bitcast(U32).rearrange("p (r i h) -> p i r h", r=PHASES, h=2),
-                in_=entries(c, 0),
-            )
+                gather(1, c * CHUNK, CHUNK, late[c])
+
+        def both(c, back):
+            col = early[c] - back
+            pitch = late[c] - early[c]
+            return listed[:, col : col + 2 * pitch].bitcast(U32).rearrange("p (h x) -> p h x", h=2)[:, :, 0:CHUNK]
+
+        def weave(c):
+            tag = "slot0" if c == CHUNKS - 1 else f"body{c}"
+            body[c] = keep.tile([P, 2 * CHUNK], I32, name=f"body{c}", tag=tag, align_bytes=64)
+            if c < SHIFTED:
+                nc.scalar.copy(
+                    out=body[c][:].bitcast(U32).rearrange("p (g r i h) -> p g i r h", g=4, r=4, h=2),
+                    in_=both(c, 0).rearrange("p h (i g r) -> p g i r h", g=4, r=4),
+                )
+            else:
+                nc.scalar.copy(
+                    out=body[c][:].bitcast(U32).rearrange("p (r i h) -> p i r h", r=RUNS, h=2),
+                    in_=both(c, 0).rearrange("p h (i r) -> p i r h", r=RUNS),
+                )
 
         def weave_halo(c):
-            tag = "slot0" if c == CHUNKS - 1 else f"halo{c}"
-            halo.append(keep.tile([P, 2 * HALO * RUN], I32, name=f"halo{c}", tag=tag, align_bytes=64))
+            tag = "slot1" if c == CHUNKS - 1 else f"halo{c}"
+            halo[c] = keep.tile([P, 2 * OVER * RUN], I32, name=f"halo{c}", tag=tag, align_bytes=64)
             nc.scalar.copy(
-                out=halo[c][:].bitcast(U32).rearrange("p (s i h) -> p i s h", s=HALO, h=2),
-                in_=entries(c, HALO)[:, :, 0:HALO, :],
+                out=halo[c][:].bitcast(U32).rearrange("p (s i h) -> p i s h", s=OVER, h=2),
+                in_=both(c, OVER).rearrange("p h (i r) -> p i r h", r=RUNS)[:, :, 0:OVER, :],
             )
+
+        for piece in CASTS[0]:
+            cast(0, raws0, *piece)
+        gather(0, 0, CHUNK, early[0])
+        gather(0, CHUNK, S - CHUNK, early[1])
+        for piece in CASTS[1][0:2]:
+            cast(1, raws1, *piece)
+        gather_plane(0)
+        for piece in CASTS[1][2:]:
+            cast(1, raws1, *piece)
+        x_scales = [keep.tile([P, widths[c]], U8, name=f"x_scales{c}", align_bytes=64) for c in range(CHUNKS)]
+        nc.vector.memset(x_scales[0][:, CHUNK:].bitcast(I32), 0)
+
+        out_rows = out.rearrange("(m p) s -> p m s", p=P)
+        accs = [[psum.tile([P, BANK], F32, name=f"acc{c}_{m}") for m in range(M_TILES)] for c in range(CHUNKS)]
+
+        for c in range(SHIFTED):
+            for m in range(M_TILES):
+                width = OPEN_N[c]
+                nc.tensor.matmul_mx(
+                    out=accs[c][m][:, BANK - width : BANK],
+                    lhsT=w_codes[TAPS - 1][:, 0:P].bitcast(FP8X4),
+                    lhsT_scale=x_scales[0][:, CHUNK : CHUNK + P],
+                    rhs=x_codes[0][:, CHUNK : CHUNK + width].bitcast(FP8X4),
+                    rhs_scale=x_scales[0][:, CHUNK : CHUNK + width],
+                    start=True,
+                    stop=False,
+                )
 
         def quantize(c, src, a, b):
             nc.vector.quantize_mx(
-                out=x_codes[c][:, a:b].bitcast(FP8X4), scales=x_scales[c][:, a:b], in_=src.bitcast(BF16)
+                out=x_codes[c][:, a:b].bitcast(FP8X4), scales=x_scales[c][:, a:b], in_=src[:].bitcast(BF16)
             )
 
-        cast_half(0, raws0)
-        gather(0, 0, HALF)
-        gather(0, HALF, HALF)
-        cast_half(1, raws1)
-
-        out_rows = out.rearrange("(m p) s -> p m s", p=P)
-        accs = [
-            [psum.tile([P, WARMUP_N], F32, name=f"acc{c}_{m}") for m in range(M_TILES)] for c in range(CHUNKS)
-        ]
-
-        def tap(c, d, m, r0, r1):
-            cols = slice((HALO - d + r0) * RUN, (HALO - d + r1) * RUN)
+        def tap(c, d, m):
+            if c < SHIFTED:
+                src, dst = 0, d * LANES
+            else:
+                src, dst = (OVER - d) * RUN, 0
             m_cols = slice(m * P, (m + 1) * P)
             nc.tensor.matmul_mx(
-                out=accs[c][m][:, r0 * RUN : r1 * RUN],
+                out=accs[c][m][:, dst : dst + CHUNK],
                 lhsT=w_codes[d][:, m_cols].bitcast(FP8X4),
                 lhsT_scale=w_scales[d][:, m_cols],
-                rhs=x_codes[c][:, cols].bitcast(FP8X4),
-                rhs_scale=x_scales[c][:, cols],
-                start=(d == 0),
+                rhs=x_codes[c][:, src : src + CHUNK].bitcast(FP8X4),
+                rhs_scale=x_scales[c][:, src : src + CHUNK],
+                start=(c >= SHIFTED and d == 0),
                 stop=(d == TAPS - 1),
             )
 
-        for i in range(WARMUP):
-            nc.tensor.matmul_mx(
-                out=accs[CHUNKS - 1][M_TILES - 1][:],
-                lhsT=w_codes[TAPS - 1][:, 0:P].bitcast(FP8X4),
-                lhsT_scale=w_scales[TAPS - 1][:, 0:P],
-                rhs=w_codes[TAPS - 1][:].bitcast(FP8X4),
-                rhs_scale=w_scales[TAPS - 1][:],
-                start=True,
-                stop=True,
-            )
-
         def multiply(c):
-            quantize(c, body[c], HALO * RUN, (HALO + PHASES) * RUN)
-            quantize(c, halo[c][:], 0, HALO * RUN)
-            first = 0
-            if c == 0:
+            if c < SHIFTED:
+                quantize(c, body[c], 0, CHUNK)
                 for m in range(M_TILES):
                     for d in range(TAPS):
-                        tap(c, d, m, HALO, PHASES)
-            last = HALO if c == 0 else PHASES
-            for m in range(M_TILES):
-                tap(c, 0, m, first, last)
-            for m in range(M_TILES):
-                for d in range(1, TAPS):
-                    tap(c, d, m, first, last)
+                        tap(c, d, m)
+            else:
+                quantize(c, body[c], OVER * RUN, OVER * RUN + CHUNK)
+                quantize(c, halo[c], 0, OVER * RUN)
+                for m in range(M_TILES):
+                    tap(c, 0, m)
+                for m in range(M_TILES):
+                    for d in range(1, TAPS):
+                        tap(c, d, m)
+
+        def phases(c, m, r0, r1):
+            return accs[c][m][:, r0 * LANES : r1 * LANES].rearrange("p (r i) -> p i r", i=LANES)
+
+        def entries(c, m, r0, r1):
+            col = c * CHUNK + r0
+            return results[m][:, col : col + CHUNK].rearrange("p (i r) -> p i r", i=LANES)[:, :, 0 : r1 - r0]
+
+        def leave(c, m, engine_copy):
+            if c < SHIFTED:
+                engine_copy(out=entries(c, m, OVER, PHASES + OVER), in_=phases(c, m, OVER, PHASES + OVER))
+            else:
+                engine_copy(
+                    out=results[m][:, c * CHUNK : (c + 1) * CHUNK].rearrange("p (i r) -> p i r", r=RUNS),
+                    in_=accs[c][m][:, 0:CHUNK].rearrange("p (r i) -> p i r", r=RUNS),
+                )
 
         def store(c, m):
-            result = keep.tile([P, CHUNK], F32, name=f"result{c}_{m}", align_bytes=64)
-            leave = nc.vector.tensor_copy if m == M_TILES - 1 else nc.scalar.copy
-            leave(
-                out=result[:].rearrange("p (i r) -> p i r", r=PHASES),
-                in_=accs[c][m][:, 0:CHUNK].rearrange("p (r i) -> p i r", r=PHASES),
-            )
-            nc.sync.dma_start(out=out_rows[:, m, c * CHUNK : (c + 1) * CHUNK], in_=result[:])
+            if c < SHIFTED:
+                nc.vector.tensor_tensor(
+                    out=entries(c, m, 0, OVER), in0=phases(c, m, 0, OVER), in1=entries(c, m, 0, OVER), op=ADD
+                )
+            cols = slice(c * CHUNK, (c + 1) * CHUNK)
+            nc.sync.dma_start(out=out_rows[:, m, cols], in_=results[m][:, cols])
 
+        on_scalar, on_vector = nc.scalar.copy, nc.vector.tensor_copy
         for c in range(CHUNKS - 1):
-            gather(1, c * CHUNK, CHUNK)
-            weave_body(c)
-            weave_halo(c)
+            gather_late(c)
+            weave(c)
+        weave_halo(2)
         multiply(0)
-        gather(1, (CHUNKS - 1) * CHUNK, CHUNK)
+        gather_late(3)
         multiply(1)
-        weave_body(CHUNKS - 1)
-        store(0, 0)
-        weave_halo(CHUNKS - 1)
         multiply(2)
+        leave(0, 0, on_scalar)
+        weave(3)
+        leave(0, 1, on_vector)
+        store(0, 0)
         store(0, 1)
+        leave(1, 0, on_scalar)
+        weave_halo(3)
+        leave(1, 1, on_scalar)
+        store(1, 0)
         multiply(3)
-        for c in range(1, CHUNKS):
-            for m in range(M_TILES):
-                store(c, m)
+        leave(2, 0, on_scalar)
+        store(2, 0)
+        store(1, 1)
+        leave(2, 1, on_vector)
+        store(2, 1)
+        leave(3, 0, on_scalar)
+        store(3, 0)
+        leave(3, 1, on_vector)
+        store(3, 1)

@@ -27,11 +27,11 @@ BANK = 512
 
 LOADS = (
     ((0, 2, 0, 1024), (0, 1, 1024, 2048), (1, 2, 1024, 1536), (1, 2, 1536, 2048)),
-    ((0, 2, 0, 512), (0, 2, 512, 1024), (0, 1, 1024, 2048), (1, 2, 1024, 1536), (1, 2, 1536, 1792), (1, 2, 1792, 2048)),
+    ((0, 2, 0, 1024), (0, 1, 1024, 2048), (1, 2, 1024, 1536), (1, 2, 1536, 1792), (1, 2, 1792, 2048)),
 )
 CASTS = (
     ((0, 688, 1024), (1024, 1376, 1536), (1536, 1888, 2048)),
-    ((0, 0, 512), (512, 512, 1024), (1024, 1376, 1536), (1536, 1712, 1792), (1792, 1792, 2048)),
+    ((0, 240, 1024), (1024, 1376, 1536), (1536, 1712, 1792), (1792, 1792, 2048)),
 )
 OPEN_N = (512, 256)
 SHIFTED = 2
@@ -116,10 +116,10 @@ def tile_picked_listconv_none_e_kernel(
             else:
                 gather(1, c * CHUNK, CHUNK, late[c])
 
-        def both(c, back):
+        def both(c, back, dtype=U32):
             col = early[c] - back
             pitch = late[c] - early[c]
-            return listed[:, col : col + 2 * pitch].bitcast(U32).rearrange("p (h x) -> p h x", h=2)[:, :, 0:CHUNK]
+            return listed[:, col : col + 2 * pitch].bitcast(dtype).rearrange("p (h x) -> p h x", h=2)[:, :, 0:CHUNK]
 
         def weave(c):
             tag = "slot0" if c == CHUNKS - 1 else f"body{c}"
@@ -136,21 +136,22 @@ def tile_picked_listconv_none_e_kernel(
                 )
 
         def weave_halo(c):
-            tag = "slot1" if c == CHUNKS - 1 else f"halo{c}"
-            halo[c] = keep.tile([P, 2 * OVER * RUN], I32, name=f"halo{c}", tag=tag, align_bytes=64)
-            nc.scalar.copy(
-                out=halo[c][:].bitcast(U32).rearrange("p (s i h) -> p i s h", s=OVER, h=2),
-                in_=both(c, OVER).rearrange("p h (i r) -> p i r h", r=RUNS)[:, :, 0:OVER, :],
+            halo[c] = keep.tile([P, 2 * OVER * RUN], I32, name=f"halo{c}", align_bytes=64)
+            engine_copy = nc.vector.tensor_copy if c == CHUNKS - 1 else nc.scalar.copy
+            dtype = I32 if c == CHUNKS - 1 else U32
+            engine_copy(
+                out=halo[c][:].bitcast(dtype).rearrange("p (s i h) -> p i s h", s=OVER, h=2),
+                in_=both(c, OVER, dtype).rearrange("p h (i r) -> p i r h", r=RUNS)[:, :, 0:OVER, :],
             )
 
         for piece in CASTS[0]:
             cast(0, raws0, *piece)
         gather(0, 0, CHUNK, early[0])
         gather(0, CHUNK, S - CHUNK, early[1])
-        for piece in CASTS[1][0:2]:
+        for piece in CASTS[1][0:1]:
             cast(1, raws1, *piece)
         gather_plane(0)
-        for piece in CASTS[1][2:]:
+        for piece in CASTS[1][1:]:
             cast(1, raws1, *piece)
         x_scales = [keep.tile([P, widths[c]], U8, name=f"x_scales{c}", align_bytes=64) for c in range(CHUNKS)]
         nc.vector.memset(x_scales[0][:, CHUNK:].bitcast(I32), 0)
@@ -195,6 +196,12 @@ def tile_picked_listconv_none_e_kernel(
         def multiply(c):
             if c < SHIFTED:
                 quantize(c, body[c], 0, CHUNK)
+                for m in range(M_TILES):
+                    for d in range(TAPS):
+                        tap(c, d, m)
+            elif c == CHUNKS - 1:
+                quantize(c, halo[c], 0, OVER * RUN)
+                quantize(c, body[c], OVER * RUN, OVER * RUN + CHUNK)
                 for m in range(M_TILES):
                     for d in range(TAPS):
                         tap(c, d, m)
@@ -245,8 +252,8 @@ def tile_picked_listconv_none_e_kernel(
         leave(0, 1, on_vector)
         store(0, 0)
         store(0, 1)
-        leave(1, 0, on_scalar)
         weave_halo(3)
+        leave(1, 0, on_scalar)
         leave(1, 1, on_scalar)
         store(1, 0)
         multiply(3)

@@ -26,11 +26,11 @@ M_TILES = N // P
 BANK = 512
 
 LOADS = (
-    ((0, 2, 0, 1024), (0, 1, 1024, 2048), (1, 2, 1024, 1536), (1, 2, 1536, 2048)),
+    ((0, 1, 0, 2048), (1, 2, 0, 1280), (1, 2, 1280, 2048)),
     ((0, 2, 0, 1024), (0, 1, 1024, 2048), (1, 2, 1024, 1536), (1, 2, 1536, 1792), (1, 2, 1792, 2048)),
 )
 CASTS = (
-    ((0, 688, 1024), (1024, 1376, 1536), (1536, 1888, 2048)),
+    ((0, 816, 1280), (1280, 1776, 2048)),
     ((0, 240, 1024), (1024, 1376, 1536), (1536, 1712, 1792), (1792, 1792, 2048)),
 )
 OPEN_N = (512, 256)
@@ -65,26 +65,36 @@ def tile_picked_listconv_none_e_kernel(
                         in_=raw[:, :, a:b].rearrange("p e t -> p t e"),
                     )
 
+        def cast_row(e, raw, t0, split, t1):
+            for engine_copy, a, b in ((nc.vector.tensor_copy, t0, split), (nc.scalar.copy, split, t1)):
+                engine_copy(
+                    out=pairs[0][:, 2 * a : 2 * b].rearrange("p (t e) -> p t e", e=2)[:, :, e], in_=raw[:, e, a:b]
+                )
+
+        planes = keep.tile([P, TAPS, N], U8, name="w_scales", align_bytes=64)
+        nc.vector.memset(planes[:].rearrange("p d n -> p (d n)").bitcast(I32), 0)
         raws0 = load_half(0)
         nc.sync.dma_start(offsets[:], offs)
+        weights = ((w1_words, w1_scales), (w2_words, w2_scales), (w3_words, w3_scales))
+        for d in reversed(range(TAPS)):
+            nc.sync.dma_start(out=planes[98:100, d, :].bitcast(I32), in_=weights[d][1][0].bitcast(I32)[14:16, :])
         raws1 = load_half(1)
 
         w_codes, w_scales = {}, {}
-        weights = ((w1_words, w1_scales), (w2_words, w2_scales), (w3_words, w3_scales))
+
+        def load_codes(d):
+            w_codes[d] = keep.tile([P, N], I32, name=f"w_codes{d}", align_bytes=64)
+            nc.sync.dma_start(out=w_codes[d][:], in_=weights[d][0][0].rearrange("p n t -> p (n t)").bitcast(I32))
+
+        load_codes(2)
         for d in reversed(range(TAPS)):
-            words, scales = weights[d]
-            codes = keep.tile([P, N], I32, name=f"w_codes{d}", align_bytes=64)
-            plane = keep.tile([P, N], U8, name=f"w_scales{d}", align_bytes=64)
-            nc.sync.dma_start(out=codes[:], in_=words[0].rearrange("p n t -> p (n t)").bitcast(I32))
-            rows = scales[0].bitcast(I32)
+            w_scales[d] = planes[:, d, :]
+            rows = weights[d][1][0].bitcast(I32)
             nc.sync.dma_start(
-                out=plane[0:98, :].bitcast(I32), in_=rows[0:14, :].unsqueeze(0).to_broadcast([7, 14, N // 4])
+                out=planes[0:98, d, :].bitcast(I32), in_=rows[0:14, :].unsqueeze(0).to_broadcast([7, 14, N // 4])
             )
-            nc.gpsimd.dma_start(
-                out=plane[98:P, :].bitcast(I32), in_=rows[14:16, :].unsqueeze(0).to_broadcast([15, 2, N // 4])
-            )
-            w_codes[d] = codes
-            w_scales[d] = plane
+        load_codes(1)
+        load_codes(0)
 
         early = (5 * CHUNK, 0, CHUNK, 2 * CHUNK)
         late = (6 * CHUNK, 3 * CHUNK, 4 * CHUNK, 5 * CHUNK)
@@ -95,9 +105,9 @@ def tile_picked_listconv_none_e_kernel(
             keep.tile([P, widths[c]], I32, name=f"x_codes{c}", tag=f"slot{c}", align_bytes=64) for c in range(CHUNKS)
         ]
         nc.vector.memset(x_codes[0][:, CHUNK:], 0)
-        results = [keep.tile([P, S], F32, name=f"result{m}", align_bytes=64) for m in range(M_TILES)]
-        for m in range(M_TILES):
-            nc.vector.memset(results[m][:, 0:OVER], 0.0)
+        result = keep.tile([P, M_TILES, S], F32, name="result", align_bytes=64)
+        results = [result[:, m, :] for m in range(M_TILES)]
+        nc.vector.memset(result[:, :, 0:OVER], 0.0)
 
         def gather(h, j0, count, col):
             window = pairs[h][:].bitcast(U32)
@@ -144,8 +154,9 @@ def tile_picked_listconv_none_e_kernel(
                 in_=both(c, OVER, dtype).rearrange("p h (i r) -> p i r h", r=RUNS)[:, :, 0:OVER, :],
             )
 
-        for piece in CASTS[0]:
-            cast(0, raws0, *piece)
+        for e in range(2):
+            for piece in CASTS[0]:
+                cast_row(e, raws0, *piece)
         gather(0, 0, CHUNK, early[0])
         gather(0, CHUNK, S - CHUNK, early[1])
         for piece in CASTS[1][0:1]:
@@ -236,7 +247,10 @@ def tile_picked_listconv_none_e_kernel(
                     out=entries(c, m, 0, OVER), in0=phases(c, m, 0, OVER), in1=entries(c, m, 0, OVER), op=ADD
                 )
             cols = slice(c * CHUNK, (c + 1) * CHUNK)
-            nc.sync.dma_start(out=out_rows[:, m, cols], in_=results[m][:, cols])
+            if c >= SHIFTED:
+                nc.sync.dma_start(out=out_rows[:, m, cols], in_=results[m][:, cols])
+            elif m == 1:
+                nc.sync.dma_start(out=out_rows[:, :, cols], in_=result[:, :, cols])
 
         on_scalar, on_vector = nc.scalar.copy, nc.vector.tensor_copy
         for c in range(CHUNKS - 1):

@@ -26,11 +26,11 @@ M_TILES = N // P
 BANK = 512
 
 LOADS = (
-    ((0, 1, 0, 2048), (1, 2, 0, 1280), (1, 2, 1280, 2048)),
+    (),
     ((0, 2, 0, 1024), (0, 1, 1024, 2048), (1, 2, 1024, 1536), (1, 2, 1536, 1792), (1, 2, 1792, 2048)),
 )
 CASTS = (
-    ((0, 816, 1280), (1280, 1776, 2048)),
+    ((0, 752, 1152), (1152, 1744, 2048)),
     ((0, 240, 1024), (1024, 1376, 1536), (1536, 1712, 1792), (1792, 1792, 2048)),
 )
 OPEN_N = (512, 256)
@@ -65,15 +65,13 @@ def tile_picked_listconv_none_e_kernel(
                         in_=raw[:, :, a:b].rearrange("p e t -> p t e"),
                     )
 
-        def cast_row(e, raw, t0, split, t1):
-            for engine_copy, a, b in ((nc.vector.tensor_copy, t0, split), (nc.scalar.copy, split, t1)):
-                engine_copy(
-                    out=pairs[0][:, 2 * a : 2 * b].rearrange("p (t e) -> p t e", e=2)[:, :, e], in_=raw[:, e, a:b]
-                )
-
         planes = keep.tile([P, TAPS, N], U8, name="w_scales", align_bytes=64)
         nc.vector.memset(planes[:].rearrange("p d n -> p (d n)").bitcast(I32), 0)
         raws0 = load_half(0)
+        early_flat = raws0[:].rearrange("p e t -> p (e t)")
+        x_flat = xT.rearrange("(p j) t -> p (j t)", j=PACK)
+        for a, b in ((0, T + 1152), (T + 1152, 2 * T)):
+            nc.sync.dma_start(out=early_flat[:, a:b], in_=x_flat[:, a:b])
         nc.sync.dma_start(offsets[:], offs)
         weights = ((w1_words, w1_scales), (w2_words, w2_scales), (w3_words, w3_scales))
         for d in reversed(range(TAPS)):
@@ -154,9 +152,8 @@ def tile_picked_listconv_none_e_kernel(
                 in_=both(c, OVER, dtype).rearrange("p h (i r) -> p i r h", r=RUNS)[:, :, 0:OVER, :],
             )
 
-        for e in range(2):
-            for piece in CASTS[0]:
-                cast_row(e, raws0, *piece)
+        for piece in CASTS[0]:
+            cast(0, raws0, *piece)
         gather(0, 0, CHUNK, early[0])
         gather(0, CHUNK, S - CHUNK, early[1])
         for piece in CASTS[1][0:1]:
@@ -247,10 +244,10 @@ def tile_picked_listconv_none_e_kernel(
                     out=entries(c, m, 0, OVER), in0=phases(c, m, 0, OVER), in1=entries(c, m, 0, OVER), op=ADD
                 )
             cols = slice(c * CHUNK, (c + 1) * CHUNK)
-            if c >= SHIFTED:
+            if (c, m) != (1, 1):
+                if (c, m) == (2, 1):
+                    cols = slice(CHUNK, 3 * CHUNK)
                 nc.sync.dma_start(out=out_rows[:, m, cols], in_=results[m][:, cols])
-            elif m == 1:
-                nc.sync.dma_start(out=out_rows[:, :, cols], in_=result[:, :, cols])
 
         on_scalar, on_vector = nc.scalar.copy, nc.vector.tensor_copy
         for c in range(CHUNKS - 1):

@@ -9,34 +9,34 @@ FLOPS = 2 * TAPS * K * N * S
 F32 = mybir.dt.float32
 BF16 = mybir.dt.bfloat16
 I32 = mybir.dt.int32
-U32 = mybir.dt.uint32
 U16 = mybir.dt.uint16
 U8 = mybir.dt.uint8
 FP8X4 = mybir.dt.float8_e4m3fn_x4
 ADD = mybir.AluOpType.add
+COPY = mybir.ActivationFunctionType.Copy
 
 P = 128
 PACK = 4
 LANES = 16
 PHASES = 16
 CHUNK = LANES * PHASES
+HALF = CHUNK // 2
 OVER = TAPS - 1
 CHUNKS = S // CHUNK
+LAST = CHUNKS - 1
 M_TILES = N // P
 BANK = 512
-
-LOADS = (
-    (),
-    ((0, 2, 0, 1024), (0, 1, 1024, 2048), (1, 2, 1024, 1536), (1, 2, 1536, 1792), (1, 2, 1792, 2048)),
-)
-CASTS = (
-    ((0, 752, 1152), (1152, 1744, 2048)),
-    ((0, 240, 1024), (1024, 1376, 1536), (1536, 1712, 1792), (1792, 1792, 2048)),
-)
-OPEN_N = (512, 256)
-SHIFTED = 2
 RUN = 64
 RUNS = CHUNK // RUN
+HALO = OVER * RUN
+OPEN_N = (256, 256, 256)
+OPEN_AT = (128, 256, 256)
+GATHERS = (
+    ((0, 512, "V"), (512, 1024, "S"),),
+    ((0, 128, "V"), (128, 256, "S"), (256, 512, "S"), (512, 768, "S"), (768, 1024, "S"),),
+    ((0, 320, "V"), (320, 1024, "S"),),
+    ((0, 128, "V"), (128, 256, "S"), (256, 512, "S"), (512, 768, "S"), (768, 1024, "S"),),
+)
 
 
 def tile_picked_listconv_none_e_kernel(
@@ -46,47 +46,31 @@ def tile_picked_listconv_none_e_kernel(
     with ExitStack() as ctx:
         keep = ctx.enter_context(tc.tile_pool(name="keep", bufs=1))
         psum = ctx.enter_context(tc.psum_pool(name="psum", bufs=1))
+        on_scalar, on_vector = nc.scalar.copy, nc.vector.tensor_copy
 
         offsets = keep.tile([P, S // 16], U16, name="offsets")
         x_rows = xT.rearrange("(p j) t -> p j t", j=PACK)
-        pairs = [keep.tile([P, 2 * T], BF16, name=f"pairs{h}", align_bytes=64) for h in range(2)]
-
-        def load_half(h):
-            raw = keep.tile([P, 2, T], F32, name=f"raw{h}", align_bytes=64)
-            for e0, e1, t0, t1 in LOADS[h]:
-                nc.sync.dma_start(out=raw[:, e0:e1, t0:t1], in_=x_rows[:, 2 * h + e0 : 2 * h + e1, t0:t1])
-            return raw
-
-        def cast(h, raw, t0, split, t1):
-            for engine_copy, a, b in ((nc.vector.tensor_copy, t0, split), (nc.scalar.copy, split, t1)):
-                if a < b:
-                    engine_copy(
-                        out=pairs[h][:, 2 * a : 2 * b].rearrange("p (t e) -> p t e", e=2),
-                        in_=raw[:, :, a:b].rearrange("p e t -> p t e"),
-                    )
-
+        raw = [keep.tile([P, T], F32, name=f"raw{t}", tag=f"row{t}", align_bytes=64) for t in range(PACK)]
+        weights = ((w1_words, w1_scales), (w2_words, w2_scales), (w3_words, w3_scales))
         planes = keep.tile([P, TAPS, N], U8, name="w_scales", align_bytes=64)
         nc.vector.memset(planes[:].rearrange("p d n -> p (d n)").bitcast(I32), 0)
-        raws0 = load_half(0)
-        early_flat = raws0[:].rearrange("p e t -> p (e t)")
-        x_flat = xT.rearrange("(p j) t -> p (j t)", j=PACK)
-        for a, b in ((0, T + 1152), (T + 1152, 2 * T)):
-            nc.sync.dma_start(out=early_flat[:, a:b], in_=x_flat[:, a:b])
-        nc.sync.dma_start(offsets[:], offs)
-        weights = ((w1_words, w1_scales), (w2_words, w2_scales), (w3_words, w3_scales))
-        for d in reversed(range(TAPS)):
-            nc.sync.dma_start(out=planes[98:100, d, :].bitcast(I32), in_=weights[d][1][0].bitcast(I32)[14:16, :])
-        raws1 = load_half(1)
+        w_codes = [keep.tile([P, N], I32, name=f"w_codes{d}", align_bytes=64) for d in range(TAPS)]
 
-        w_codes, w_scales = {}, {}
+        def load_row(t):
+            nc.sync.dma_start(out=raw[t][:], in_=x_rows[:, t, :])
 
         def load_codes(d):
-            w_codes[d] = keep.tile([P, N], I32, name=f"w_codes{d}", align_bytes=64)
             nc.sync.dma_start(out=w_codes[d][:], in_=weights[d][0][0].rearrange("p n t -> p (n t)").bitcast(I32))
 
+        load_row(0)
+        nc.sync.dma_start(offsets[:], offs)
+        load_row(1)
+        for d in range(TAPS):
+            nc.sync.dma_start(out=planes[98:100, d, :].bitcast(I32), in_=weights[d][1][0].bitcast(I32)[14:16, :])
+        load_row(2)
+        load_row(3)
         load_codes(2)
         for d in reversed(range(TAPS)):
-            w_scales[d] = planes[:, d, :]
             rows = weights[d][1][0].bitcast(I32)
             nc.sync.dma_start(
                 out=planes[0:98, d, :].bitcast(I32), in_=rows[0:14, :].unsqueeze(0).to_broadcast([7, 14, N // 4])
@@ -94,133 +78,95 @@ def tile_picked_listconv_none_e_kernel(
         load_codes(1)
         load_codes(0)
 
-        early = (5 * CHUNK, 0, CHUNK, 2 * CHUNK)
-        late = (6 * CHUNK, 3 * CHUNK, 4 * CHUNK, 5 * CHUNK)
-        listed = keep.tile([P, 8 * CHUNK], I32, name="listed", align_bytes=64)
-        body, halo = {}, {}
-        widths = (CHUNK + BANK, CHUNK, CHUNK + OVER * RUN, CHUNK + OVER * RUN)
-        x_codes = [
-            keep.tile([P, widths[c]], I32, name=f"x_codes{c}", tag=f"slot{c}", align_bytes=64) for c in range(CHUNKS)
-        ]
+        width = [HALO + CHUNK if c == LAST else CHUNK for c in range(CHUNKS)]
+        picked = [keep.tile([P, 2, S], BF16, name=f"picked{h}", tag=f"picked{h}", align_bytes=64) for h in range(2)]
+        body = [keep.tile([P, PACK * width[c]], BF16, name=f"body{c}", tag=f"body{c}", align_bytes=64) for c in range(CHUNKS)]
+        x_codes = {0: keep.tile([P, CHUNK + max(OPEN_N)], I32, name="x_codes0", align_bytes=64)}
+        x_scales = {}
         nc.vector.memset(x_codes[0][:, CHUNK:], 0)
         result = keep.tile([P, M_TILES, S], F32, name="result", align_bytes=64)
         results = [result[:, m, :] for m in range(M_TILES)]
-        nc.vector.memset(result[:, :, 0:OVER], 0.0)
+        zeros = keep.tile([P, M_TILES, OVER], F32, name="zeros")
+        nc.vector.memset(zeros[:], 0.0)
+        carry = [
+            keep.tile([P, LANES, OVER], F32, name=f"carry{m}", tag=("x_codes3", "carry1")[m], align_bytes=64)
+            for m in range(M_TILES)
+        ]
+        for m in range(M_TILES):
+            nc.scalar.activation(out=carry[m][:, 0, :], in_=zeros[:, m, :], func=COPY)
 
-        def gather(h, j0, count, col):
-            window = pairs[h][:].bitcast(U32)
-            nc.vector.tensor_copy(
-                out=listed[:, col : col + count].bitcast(U32),
-                in_=window.indirect(offsets[:, j0 // 16 : (j0 + count) // 16]),
-            )
+        def gather_row(t):
+            for a, b, engine in GATHERS[t]:
+                dst = picked[t // 2][:, t % 2, a:b]
+                src = raw[t][:].indirect(offsets[:, a // 16 : b // 16])
+                if engine == "V":
+                    nc.vector.tensor_copy(out=dst, in_=src)
+                else:
+                    nc.scalar.activation(out=dst, in_=src, func=COPY)
 
-        def gather_plane(e):
-            halves = listed[:, late[0] : late[0] + CHUNK].bitcast(BF16).rearrange("p (j e) -> p j e", e=2)
-            nc.vector.tensor_copy(out=halves[:, :, e], in_=raws1[:, e, :].indirect(offsets[:, 0 : CHUNK // 16]))
-
-        def gather_late(c):
-            if c == 0:
-                gather_plane(1)
-            else:
-                gather(1, c * CHUNK, CHUNK, late[c])
-
-        def both(c, back, dtype=U32):
-            col = early[c] - back
-            pitch = late[c] - early[c]
-            return listed[:, col : col + 2 * pitch].bitcast(dtype).rearrange("p (h x) -> p h x", h=2)[:, :, 0:CHUNK]
-
-        def weave(c):
-            tag = "slot0" if c == CHUNKS - 1 else f"body{c}"
-            body[c] = keep.tile([P, 2 * CHUNK], I32, name=f"body{c}", tag=tag, align_bytes=64)
-            if c < SHIFTED:
-                nc.scalar.copy(
-                    out=body[c][:].bitcast(U32).rearrange("p (g r i h) -> p g i r h", g=4, r=4, h=2),
-                    in_=both(c, 0).rearrange("p h (i g r) -> p g i r h", g=4, r=4),
+        def fill(c, h, part=slice(0, 4), engine_copy=on_vector):
+            pair = slice(2 * h, 2 * h + 2)
+            src = picked[h][:, :, c * CHUNK : (c + 1) * CHUNK]
+            if c < LAST:
+                engine_copy(
+                    out=body[c][:].rearrange("p (g r i t) -> p g i r t", g=4, r=4, t=PACK)[:, part, :, :, pair],
+                    in_=src.rearrange("p u (i g r) -> p g i r u", g=4, r=4)[:, part],
                 )
             else:
-                nc.scalar.copy(
-                    out=body[c][:].bitcast(U32).rearrange("p (r i h) -> p i r h", r=RUNS, h=2),
-                    in_=both(c, 0).rearrange("p h (i r) -> p i r h", r=RUNS),
+                engine_copy(
+                    out=body[c][:, PACK * HALO :].rearrange("p (r i t) -> p i r t", r=RUNS, t=PACK)[:, :, part, pair],
+                    in_=src.rearrange("p u (i r) -> p i r u", r=RUNS)[:, :, part],
                 )
 
-        def weave_halo(c):
-            halo[c] = keep.tile([P, 2 * OVER * RUN], I32, name=f"halo{c}", align_bytes=64)
-            engine_copy = nc.vector.tensor_copy if c == CHUNKS - 1 else nc.scalar.copy
-            dtype = I32 if c == CHUNKS - 1 else U32
+        def fill_halo(h, engine_copy):
+            pair = slice(2 * h, 2 * h + 2)
+            back = picked[h][:, :, LAST * CHUNK - OVER : S - OVER]
             engine_copy(
-                out=halo[c][:].bitcast(dtype).rearrange("p (s i h) -> p i s h", s=OVER, h=2),
-                in_=both(c, OVER, dtype).rearrange("p h (i r) -> p i r h", r=RUNS)[:, :, 0:OVER, :],
+                out=body[LAST][:, 0 : PACK * HALO].rearrange("p (r i t) -> p i r t", r=OVER, t=PACK)[:, :, :, pair],
+                in_=back.rearrange("p u (i r) -> p i r u", r=RUNS)[:, :, 0:OVER, :],
             )
-
-        for piece in CASTS[0]:
-            cast(0, raws0, *piece)
-        gather(0, 0, CHUNK, early[0])
-        gather(0, CHUNK, S - CHUNK, early[1])
-        for piece in CASTS[1][0:1]:
-            cast(1, raws1, *piece)
-        gather_plane(0)
-        for piece in CASTS[1][1:]:
-            cast(1, raws1, *piece)
-        x_scales = [keep.tile([P, widths[c]], U8, name=f"x_scales{c}", align_bytes=64) for c in range(CHUNKS)]
-        nc.vector.memset(x_scales[0][:, CHUNK:].bitcast(I32), 0)
 
         out_rows = out.rearrange("(m p) s -> p m s", p=P)
         accs = [[psum.tile([P, BANK], F32, name=f"acc{c}_{m}") for m in range(M_TILES)] for c in range(CHUNKS)]
 
-        for c in range(SHIFTED):
-            for m in range(M_TILES):
-                width = OPEN_N[c]
-                nc.tensor.matmul_mx(
-                    out=accs[c][m][:, BANK - width : BANK],
-                    lhsT=w_codes[TAPS - 1][:, 0:P].bitcast(FP8X4),
-                    lhsT_scale=x_scales[0][:, CHUNK : CHUNK + P],
-                    rhs=x_codes[0][:, CHUNK : CHUNK + width].bitcast(FP8X4),
-                    rhs_scale=x_scales[0][:, CHUNK : CHUNK + width],
-                    start=True,
-                    stop=False,
-                )
+        def open_banks():
+            x_scales[0] = keep.tile([P, CHUNK + max(OPEN_N)], U8, name="x_scales0", tag="picked0", align_bytes=64)
+            nc.vector.memset(x_scales[0][:, CHUNK:].bitcast(I32), 0)
+            for c in range(LAST):
+                for m in range(M_TILES):
+                    nc.tensor.matmul_mx(
+                        out=accs[c][m][:, OPEN_AT[c] : OPEN_AT[c] + OPEN_N[c]],
+                        lhsT=x_codes[0][:, CHUNK : CHUNK + P].bitcast(FP8X4),
+                        lhsT_scale=x_scales[0][:, CHUNK : CHUNK + P],
+                        rhs=x_codes[0][:, CHUNK : CHUNK + OPEN_N[c]].bitcast(FP8X4),
+                        rhs_scale=x_scales[0][:, CHUNK : CHUNK + OPEN_N[c]],
+                        start=True,
+                        stop=False,
+                    )
 
-        def quantize(c, src, a, b):
+        def quantize(c, a=0, b=None):
+            if c not in x_codes:
+                x_codes[c] = keep.tile([P, width[c]], I32, name=f"x_codes{c}", tag=f"x_codes{c}", align_bytes=64)
+                x_scales[c] = keep.tile([P, width[c]], U8, name=f"x_scales{c}", tag=f"x_scales{c}", align_bytes=64)
+            b = width[c] if b is None else b
             nc.vector.quantize_mx(
-                out=x_codes[c][:, a:b].bitcast(FP8X4), scales=x_scales[c][:, a:b], in_=src[:].bitcast(BF16)
+                out=x_codes[c][:, a:b].bitcast(FP8X4), scales=x_scales[c][:, a:b], in_=body[c][:, PACK * a : PACK * b]
             )
 
-        def tap(c, d, m):
-            if c < SHIFTED:
-                src, dst = 0, d * LANES
-            else:
-                src, dst = (OVER - d) * RUN, 0
-            m_cols = slice(m * P, (m + 1) * P)
-            nc.tensor.matmul_mx(
-                out=accs[c][m][:, dst : dst + CHUNK],
-                lhsT=w_codes[d][:, m_cols].bitcast(FP8X4),
-                lhsT_scale=w_scales[d][:, m_cols],
-                rhs=x_codes[c][:, src : src + CHUNK].bitcast(FP8X4),
-                rhs_scale=x_scales[c][:, src : src + CHUNK],
-                start=(c >= SHIFTED and d == 0),
-                stop=(d == TAPS - 1),
-            )
-
-        def multiply(c):
-            if c < SHIFTED:
-                quantize(c, body[c], 0, CHUNK)
-                for m in range(M_TILES):
-                    for d in range(TAPS):
-                        tap(c, d, m)
-            elif c == CHUNKS - 1:
-                quantize(c, halo[c], 0, OVER * RUN)
-                quantize(c, body[c], OVER * RUN, OVER * RUN + CHUNK)
-                for m in range(M_TILES):
-                    for d in range(TAPS):
-                        tap(c, d, m)
-            else:
-                quantize(c, body[c], OVER * RUN, OVER * RUN + CHUNK)
-                quantize(c, halo[c], 0, OVER * RUN)
-                for m in range(M_TILES):
-                    tap(c, 0, m)
-                for m in range(M_TILES):
-                    for d in range(1, TAPS):
-                        tap(c, d, m)
+        def multiply(c, a=0, b=CHUNK, tiles=range(M_TILES)):
+            for m in tiles:
+                for d in range(TAPS):
+                    src, dst = (0, d * LANES) if c < LAST else ((OVER - d) * RUN, 0)
+                    m_cols = slice(m * P, (m + 1) * P)
+                    nc.tensor.matmul_mx(
+                        out=accs[c][m][:, dst + a : dst + b],
+                        lhsT=w_codes[d][:, m_cols].bitcast(FP8X4),
+                        lhsT_scale=planes[:, d, m_cols],
+                        rhs=x_codes[c][:, src + a : src + b].bitcast(FP8X4),
+                        rhs_scale=x_scales[c][:, src + a : src + b],
+                        start=(c == LAST and a == 0 and d == 0),
+                        stop=(b == CHUNK and d == TAPS - 1),
+                    )
 
         def phases(c, m, r0, r1):
             return accs[c][m][:, r0 * LANES : r1 * LANES].rearrange("p (r i) -> p i r", i=LANES)
@@ -230,7 +176,9 @@ def tile_picked_listconv_none_e_kernel(
             return results[m][:, col : col + CHUNK].rearrange("p (i r) -> p i r", i=LANES)[:, :, 0 : r1 - r0]
 
         def leave(c, m, engine_copy):
-            if c < SHIFTED:
+            if c == 0:
+                engine_copy(out=carry[m][:, 1:LANES, :], in_=phases(c, m, PHASES, PHASES + OVER)[:, 0 : LANES - 1, :])
+            if c < LAST:
                 engine_copy(out=entries(c, m, OVER, PHASES + OVER), in_=phases(c, m, OVER, PHASES + OVER))
             else:
                 engine_copy(
@@ -238,42 +186,47 @@ def tile_picked_listconv_none_e_kernel(
                     in_=accs[c][m][:, 0:CHUNK].rearrange("p (r i) -> p i r", r=RUNS),
                 )
 
-        def store(c, m):
-            if c < SHIFTED:
-                nc.vector.tensor_tensor(
-                    out=entries(c, m, 0, OVER), in0=phases(c, m, 0, OVER), in1=entries(c, m, 0, OVER), op=ADD
-                )
-            cols = slice(c * CHUNK, (c + 1) * CHUNK)
-            if (c, m) != (1, 1):
-                if (c, m) == (2, 1):
-                    cols = slice(CHUNK, 3 * CHUNK)
-                nc.sync.dma_start(out=out_rows[:, m, cols], in_=results[m][:, cols])
+        def join(c, m):
+            before = carry[m][:] if c == 0 else entries(c, m, 0, OVER)
+            nc.vector.tensor_tensor(out=entries(c, m, 0, OVER), in0=phases(c, m, 0, OVER), in1=before, op=ADD)
 
-        on_scalar, on_vector = nc.scalar.copy, nc.vector.tensor_copy
-        for c in range(CHUNKS - 1):
-            gather_late(c)
-            weave(c)
-        weave_halo(2)
-        multiply(0)
-        gather_late(3)
-        multiply(1)
-        multiply(2)
-        leave(0, 0, on_scalar)
-        weave(3)
-        leave(0, 1, on_vector)
-        store(0, 0)
-        store(0, 1)
-        weave_halo(3)
-        leave(1, 0, on_scalar)
-        leave(1, 1, on_scalar)
-        store(1, 0)
-        multiply(3)
-        leave(2, 0, on_scalar)
-        store(2, 0)
-        store(1, 1)
-        leave(2, 1, on_vector)
-        store(2, 1)
-        leave(3, 0, on_scalar)
-        store(3, 0)
-        leave(3, 1, on_vector)
-        store(3, 1)
+        def store(m, c0, c1):
+            cols = slice(c0 * CHUNK, c1 * CHUNK)
+            nc.sync.dma_start(out=out_rows[:, m, cols], in_=results[m][:, cols])
+
+        def drain(c):
+            for m in range(M_TILES):
+                leave(c, m, on_vector if (c, m) == (LAST, 1) else on_scalar)
+                if c < LAST:
+                    join(c, m)
+                store(m, c, c + 1)
+
+        gather_row(0)
+        gather_row(1)
+        for c in range(CHUNKS):
+            fill(c, 0)
+        fill_halo(0, on_vector)
+        gather_row(2)
+        open_banks()
+        gather_row(3)
+        for c in range(CHUNKS):
+            if c == LAST:
+                fill_halo(1, on_scalar)
+            fill(c, 1, slice(0, 2))
+            fill(c, 1, slice(2, 4))
+            if c == 0:
+                quantize(c, 0, HALF)
+                quantize(c, HALF, CHUNK)
+                multiply(c, 0, HALF)
+                multiply(c, HALF, CHUNK)
+            elif c < LAST:
+                quantize(c)
+                multiply(c)
+            else:
+                quantize(c, 0, CHUNK)
+                quantize(c, CHUNK, CHUNK + HALO)
+                multiply(c, 0, HALF)
+                multiply(c, HALF, CHUNK)
+            if c > 0:
+                drain(c - 1)
+        drain(LAST)

@@ -35,7 +35,7 @@ GATHERS = (
     ((0, 512, "V"), (512, 1024, "S"),),
     ((0, 128, "V"), (128, 256, "S"), (256, 512, "S"), (512, 768, "S"), (768, 1024, "S"),),
     ((0, 320, "V"), (320, 1024, "S"),),
-    ((0, 128, "V"), (128, 256, "S"), (256, 512, "S"), (512, 768, "S"), (768, 1024, "S"),),
+    ((0, 128, "V"), (128, 256, "S"), (256, 352, "V"), (352, 512, "S"), (512, 768, "S"), (768, 1024, "S"),),
 )
 
 
@@ -109,21 +109,21 @@ def tile_picked_listconv_none_e_kernel(
             src = picked[h][:, :, c * CHUNK : (c + 1) * CHUNK]
             if c < LAST:
                 engine_copy(
-                    out=body[c][:].rearrange("p (g r i t) -> p g i r t", g=4, r=4, t=PACK)[:, part, :, :, pair],
-                    in_=src.rearrange("p u (i g r) -> p g i r u", g=4, r=4)[:, part],
+                    out=body[c][:].rearrange("p (r i e t) -> p i r e t", r=PHASES, e=2, t=PACK)[:, :, 4 * part.start : 4 * part.stop, :, pair],
+                    in_=src.rearrange("p u (i e r) -> p i r e u", e=2, r=PHASES)[:, :, 4 * part.start : 4 * part.stop],
                 )
             else:
                 engine_copy(
-                    out=body[c][:, PACK * HALO :].rearrange("p (r i t) -> p i r t", r=RUNS, t=PACK)[:, :, part, pair],
-                    in_=src.rearrange("p u (i r) -> p i r u", r=RUNS)[:, :, part],
+                    out=body[c][:, PACK * HALO :].rearrange("p (r i e t) -> p i r e t", r=RUNS, e=2, t=PACK)[:, :, part, :, pair],
+                    in_=src.rearrange("p u (i e r) -> p i r e u", e=2, r=RUNS)[:, :, part],
                 )
 
         def fill_halo(h, engine_copy):
             pair = slice(2 * h, 2 * h + 2)
             back = picked[h][:, :, LAST * CHUNK - OVER : S - OVER]
             engine_copy(
-                out=body[LAST][:, 0 : PACK * HALO].rearrange("p (r i t) -> p i r t", r=OVER, t=PACK)[:, :, :, pair],
-                in_=back.rearrange("p u (i r) -> p i r u", r=RUNS)[:, :, 0:OVER, :],
+                out=body[LAST][:, 0 : PACK * HALO].rearrange("p (r i e t) -> p i r e t", r=OVER, e=2, t=PACK)[:, :, :, :, pair],
+                in_=back.rearrange("p u (i e r) -> p i r e u", e=2, r=RUNS)[:, :, 0:OVER],
             )
 
         out_rows = out.rearrange("(m p) s -> p m s", p=P)

@@ -88,12 +88,7 @@ def tile_picked_listconv_none_e_kernel(
         results = [result[:, m, :] for m in range(M_TILES)]
         zeros = keep.tile([P, M_TILES, OVER], F32, name="zeros")
         nc.vector.memset(zeros[:], 0.0)
-        carry = [
-            keep.tile([P, LANES, OVER], F32, name=f"carry{m}", tag=("x_codes3", "carry1")[m], align_bytes=64)
-            for m in range(M_TILES)
-        ]
-        for m in range(M_TILES):
-            nc.scalar.activation(out=carry[m][:, 0, :], in_=zeros[:, m, :], func=COPY)
+        nc.scalar.activation(out=result[:, :, 0:OVER], in_=zeros[:], func=COPY)
 
         def gather_row(t):
             for a, b, engine in GATHERS[t]:
@@ -176,8 +171,6 @@ def tile_picked_listconv_none_e_kernel(
             return results[m][:, col : col + CHUNK].rearrange("p (i r) -> p i r", i=LANES)[:, :, 0 : r1 - r0]
 
         def leave(c, m, engine_copy):
-            if c == 0:
-                engine_copy(out=carry[m][:, 1:LANES, :], in_=phases(c, m, PHASES, PHASES + OVER)[:, 0 : LANES - 1, :])
             if c < LAST:
                 engine_copy(out=entries(c, m, OVER, PHASES + OVER), in_=phases(c, m, OVER, PHASES + OVER))
             else:
@@ -187,8 +180,7 @@ def tile_picked_listconv_none_e_kernel(
                 )
 
         def join(c, m):
-            before = carry[m][:] if c == 0 else entries(c, m, 0, OVER)
-            nc.vector.tensor_tensor(out=entries(c, m, 0, OVER), in0=phases(c, m, 0, OVER), in1=before, op=ADD)
+            nc.vector.tensor_tensor(out=entries(c, m, 0, OVER), in0=phases(c, m, 0, OVER), in1=entries(c, m, 0, OVER), op=ADD)
 
         def store(m, c0, c1):
             cols = slice(c0 * CHUNK, c1 * CHUNK)

@@ -19,6 +19,7 @@ P = 128
 PACK = 4
 LANES = 16
 PHASES = 16
+LINE = 4
 CHUNK = LANES * PHASES
 HALF = CHUNK // 2
 OVER = TAPS - 1
@@ -86,9 +87,9 @@ def tile_picked_listconv_none_e_kernel(
         nc.vector.memset(x_codes[0][:, CHUNK:], 0)
         result = keep.tile([P, M_TILES, S], F32, name="result", align_bytes=64)
         results = [result[:, m, :] for m in range(M_TILES)]
-        zeros = keep.tile([P, M_TILES, OVER], F32, name="zeros")
+        zeros = keep.tile([P, M_TILES, LINE], F32, name="zeros")
         nc.vector.memset(zeros[:], 0.0)
-        nc.scalar.activation(out=result[:, :, 0:OVER], in_=zeros[:], func=COPY)
+        nc.scalar.activation(out=result[:, :, 0:LINE], in_=zeros[:], func=COPY)
 
         def gather_row(t):
             for a, b, engine in GATHERS[t]:
@@ -172,7 +173,10 @@ def tile_picked_listconv_none_e_kernel(
 
         def leave(c, m, engine_copy):
             if c < LAST:
-                engine_copy(out=entries(c, m, OVER, PHASES + OVER), in_=phases(c, m, OVER, PHASES + OVER))
+                engine_copy(
+                    out=results[m][:, c * CHUNK + LINE : (c + 1) * CHUNK + LINE].rearrange("p (i q r) -> p q i r", i=LANES, r=LINE),
+                    in_=accs[c][m][:, LINE * LANES : LINE * LANES + CHUNK].rearrange("p (q r i) -> p q i r", r=LINE, i=LANES),
+                )
             else:
                 engine_copy(
                     out=results[m][:, c * CHUNK : (c + 1) * CHUNK].rearrange("p (i r) -> p i r", r=RUNS),
@@ -180,7 +184,7 @@ def tile_picked_listconv_none_e_kernel(
                 )
 
         def join(c, m):
-            nc.vector.tensor_tensor(out=entries(c, m, 0, OVER), in0=phases(c, m, 0, OVER), in1=entries(c, m, 0, OVER), op=ADD)
+            nc.vector.tensor_tensor(out=entries(c, m, 0, LINE), in0=phases(c, m, 0, LINE), in1=entries(c, m, 0, LINE), op=ADD)
 
         def store(m, c0, c1):
             cols = slice(c0 * CHUNK, c1 * CHUNK)

@@ -30,8 +30,8 @@ BANK = 512
 RUN = 64
 RUNS = CHUNK // RUN
 HALO = OVER * RUN
-OPEN_N = (256, 256, 256)
-OPEN_AT = (128, 256, 256)
+OPENS = (((0, 128), (128, 256)), ((256, 256),), ((256, 128),))
+OPEN_MAX = 256
 GATHERS = (
     ((0, 512, "V"), (512, 1024, "S"),),
     ((0, 128, "V"), (128, 256, "S"), (256, 512, "S"), (512, 768, "S"), (768, 1024, "S"),),
@@ -76,13 +76,13 @@ def tile_picked_listconv_none_e_kernel(
             nc.sync.dma_start(
                 out=planes[0:98, d, :].bitcast(I32), in_=rows[0:14, :].unsqueeze(0).to_broadcast([7, 14, N // 4])
             )
-        load_codes(1)
-        load_codes(0)
+            if d < OVER:
+                load_codes(d)
 
         width = [HALO + CHUNK if c == LAST else CHUNK for c in range(CHUNKS)]
         picked = [keep.tile([P, 2, S], BF16, name=f"picked{h}", tag=f"picked{h}", align_bytes=64) for h in range(2)]
         body = [keep.tile([P, PACK * width[c]], BF16, name=f"body{c}", tag=f"body{c}", align_bytes=64) for c in range(CHUNKS)]
-        x_codes = {0: keep.tile([P, CHUNK + max(OPEN_N)], I32, name="x_codes0", align_bytes=64)}
+        x_codes = {0: keep.tile([P, CHUNK + OPEN_MAX], I32, name="x_codes0", align_bytes=64)}
         x_scales = {}
         nc.vector.memset(x_codes[0][:, CHUNK:], 0)
         result = keep.tile([P, M_TILES, S], F32, name="result", align_bytes=64)
@@ -126,19 +126,20 @@ def tile_picked_listconv_none_e_kernel(
         accs = [[psum.tile([P, BANK], F32, name=f"acc{c}_{m}") for m in range(M_TILES)] for c in range(CHUNKS)]
 
         def open_banks():
-            x_scales[0] = keep.tile([P, CHUNK + max(OPEN_N)], U8, name="x_scales0", tag="picked0", align_bytes=64)
+            x_scales[0] = keep.tile([P, CHUNK + OPEN_MAX], U8, name="x_scales0", tag="picked0", align_bytes=64)
             nc.vector.memset(x_scales[0][:, CHUNK:].bitcast(I32), 0)
             for c in range(LAST):
                 for m in range(M_TILES):
-                    nc.tensor.matmul_mx(
-                        out=accs[c][m][:, OPEN_AT[c] : OPEN_AT[c] + OPEN_N[c]],
-                        lhsT=x_codes[0][:, CHUNK : CHUNK + P].bitcast(FP8X4),
-                        lhsT_scale=x_scales[0][:, CHUNK : CHUNK + P],
-                        rhs=x_codes[0][:, CHUNK : CHUNK + OPEN_N[c]].bitcast(FP8X4),
-                        rhs_scale=x_scales[0][:, CHUNK : CHUNK + OPEN_N[c]],
-                        start=True,
-                        stop=False,
-                    )
+                    for k, (at, n) in enumerate(OPENS[c]):
+                        nc.tensor.matmul_mx(
+                            out=accs[c][m][:, at : at + n],
+                            lhsT=x_codes[0][:, CHUNK : CHUNK + P].bitcast(FP8X4),
+                            lhsT_scale=x_scales[0][:, CHUNK : CHUNK + P],
+                            rhs=x_codes[0][:, CHUNK : CHUNK + n].bitcast(FP8X4),
+                            rhs_scale=x_scales[0][:, CHUNK : CHUNK + n],
+                            start=(k == 0),
+                            stop=False,
+                        )
 
         def quantize(c, a=0, b=None):
             if c not in x_codes:
@@ -149,9 +150,9 @@ def tile_picked_listconv_none_e_kernel(
                 out=x_codes[c][:, a:b].bitcast(FP8X4), scales=x_scales[c][:, a:b], in_=body[c][:, PACK * a : PACK * b]
             )
 
-        def multiply(c, a=0, b=CHUNK, tiles=range(M_TILES)):
-            for m in tiles:
-                for d in range(TAPS):
+        def multiply(c, a=0, b=CHUNK, taps=range(TAPS), closes=True):
+            for m in range(M_TILES):
+                for d in taps:
                     src, dst = (0, d * LANES) if c < LAST else ((OVER - d) * RUN, 0)
                     m_cols = slice(m * P, (m + 1) * P)
                     nc.tensor.matmul_mx(
@@ -161,7 +162,7 @@ def tile_picked_listconv_none_e_kernel(
                         rhs=x_codes[c][:, src + a : src + b].bitcast(FP8X4),
                         rhs_scale=x_scales[c][:, src + a : src + b],
                         start=(c == LAST and a == 0 and d == 0),
-                        stop=(b == CHUNK and d == TAPS - 1),
+                        stop=(closes and d == taps[-1]),
                     )
 
         def phases(c, m, r0, r1):
@@ -184,7 +185,12 @@ def tile_picked_listconv_none_e_kernel(
                 )
 
         def join(c, m):
-            nc.vector.tensor_tensor(out=entries(c, m, 0, LINE), in0=phases(c, m, 0, LINE), in1=entries(c, m, 0, LINE), op=ADD)
+            sums = phases(c, m, 0, LINE)
+            if (c, m) == (0, 0):
+                firsts = keep.tile([P, LANES, LINE], F32, name="firsts", tag=f"x_scales{LAST}", align_bytes=64)
+                on_scalar(out=firsts[:], in_=sums)
+                sums = firsts[:]
+            nc.vector.tensor_tensor(out=entries(c, m, 0, LINE), in0=sums, in1=entries(c, m, 0, LINE), op=ADD)
 
         def store(m, c0, c1):
             cols = slice(c0 * CHUNK, c1 * CHUNK)
@@ -213,15 +219,16 @@ def tile_picked_listconv_none_e_kernel(
             if c == 0:
                 quantize(c, 0, HALF)
                 quantize(c, HALF, CHUNK)
-                multiply(c, 0, HALF)
-                multiply(c, HALF, CHUNK)
+                multiply(c, 0, HALF, (2, 1), False)
+                multiply(c, HALF, CHUNK, (2, 1), False)
+                multiply(c, 0, CHUNK, (0,))
             elif c < LAST:
                 quantize(c)
                 multiply(c)
             else:
                 quantize(c, 0, CHUNK)
                 quantize(c, CHUNK, CHUNK + HALO)
-                multiply(c, 0, HALF)
+                multiply(c, 0, HALF, closes=False)
                 multiply(c, HALF, CHUNK)
             if c > 0:
                 drain(c - 1)

@@ -185,12 +185,7 @@ def tile_picked_listconv_none_e_kernel(
                 )
 
         def join(c, m):
-            sums = phases(c, m, 0, LINE)
-            if (c, m) == (0, 0):
-                firsts = keep.tile([P, LANES, LINE], F32, name="firsts", tag=f"x_scales{LAST}", align_bytes=64)
-                on_scalar(out=firsts[:], in_=sums)
-                sums = firsts[:]
-            nc.vector.tensor_tensor(out=entries(c, m, 0, LINE), in0=sums, in1=entries(c, m, 0, LINE), op=ADD)
+            nc.vector.tensor_tensor(out=entries(c, m, 0, LINE), in0=phases(c, m, 0, LINE), in1=entries(c, m, 0, LINE), op=ADD)
 
         def store(m, c0, c1):
             cols = slice(c0 * CHUNK, c1 * CHUNK)
@@ -228,8 +223,7 @@ def tile_picked_listconv_none_e_kernel(
             else:
                 quantize(c, 0, CHUNK)
                 quantize(c, CHUNK, CHUNK + HALO)
-                multiply(c, 0, HALF, closes=False)
-                multiply(c, HALF, CHUNK)
+                multiply(c)
             if c > 0:
                 drain(c - 1)
         drain(LAST)

@@ -150,8 +150,8 @@ def tile_picked_listconv_none_e_kernel(
                 out=x_codes[c][:, a:b].bitcast(FP8X4), scales=x_scales[c][:, a:b], in_=body[c][:, PACK * a : PACK * b]
             )
 
-        def multiply(c, a=0, b=CHUNK, taps=range(TAPS), closes=True):
-            for m in range(M_TILES):
+        def multiply(c, a=0, b=CHUNK, taps=range(TAPS), closes=True, tiles=range(M_TILES)):
+            for m in tiles:
                 for d in taps:
                     src, dst = (0, d * LANES) if c < LAST else ((OVER - d) * RUN, 0)
                     m_cols = slice(m * P, (m + 1) * P)
@@ -185,7 +185,12 @@ def tile_picked_listconv_none_e_kernel(
                 )
 
         def join(c, m):
-            nc.vector.tensor_tensor(out=entries(c, m, 0, LINE), in0=phases(c, m, 0, LINE), in1=entries(c, m, 0, LINE), op=ADD)
+            sums = phases(c, m, 0, LINE)
+            if (c, m) == (0, 0):
+                firsts = keep.tile([P, LANES, LINE], F32, name="firsts", tag=f"x_scales{LAST}", align_bytes=64)
+                on_scalar(out=firsts[:], in_=sums)
+                sums = firsts[:]
+            nc.vector.tensor_tensor(out=entries(c, m, 0, LINE), in0=sums, in1=entries(c, m, 0, LINE), op=ADD)
 
         def store(m, c0, c1):
             cols = slice(c0 * CHUNK, c1 * CHUNK)
@@ -214,9 +219,10 @@ def tile_picked_listconv_none_e_kernel(
             if c == 0:
                 quantize(c, 0, HALF)
                 quantize(c, HALF, CHUNK)
-                multiply(c, 0, HALF, (2, 1), False)
-                multiply(c, HALF, CHUNK, (2, 1), False)
-                multiply(c, 0, CHUNK, (0,))
+                for m in range(M_TILES):
+                    multiply(c, 0, HALF, (2, 1), False, (m,))
+                    multiply(c, HALF, CHUNK, (2, 1), False, (m,))
+                    multiply(c, 0, CHUNK, (0,), True, (m,))
             elif c < LAST:
                 quantize(c)
                 multiply(c)

@@ -214,8 +214,11 @@ def tile_picked_listconv_none_e_kernel(
         for c in range(CHUNKS):
             if c == LAST:
                 fill_halo(1, on_scalar)
-            fill(c, 1, slice(0, 2))
-            fill(c, 1, slice(2, 4))
+            if c < LAST - 1:
+                fill(c, 1, slice(0, 2))
+                fill(c, 1, slice(2, 4))
+            else:
+                fill(c, 1)
             if c == 0:
                 quantize(c, 0, HALF)
                 quantize(c, HALF, CHUNK)
@@ -227,8 +230,7 @@ def tile_picked_listconv_none_e_kernel(
                 quantize(c)
                 multiply(c)
             else:
-                quantize(c, 0, CHUNK)
-                quantize(c, CHUNK, CHUNK + HALO)
+                quantize(c)
                 multiply(c)
             if c > 0:
                 drain(c - 1)

@@ -36,7 +36,7 @@ GATHERS = (
     ((0, 512, "V"), (512, 1024, "S"),),
     ((0, 128, "V"), (128, 256, "S"), (256, 512, "S"), (512, 768, "S"), (768, 1024, "S"),),
     ((0, 320, "V"), (320, 1024, "S"),),
-    ((0, 128, "V"), (128, 256, "S"), (256, 352, "V"), (352, 512, "S"), (512, 768, "S"), (768, 1024, "S"),),
+    ((0, 128, "V"), (128, 256, "S"), (256, 384, "V"), (384, 512, "S"), (512, 768, "S"), (768, 1024, "S"),),
 )
 
 
@@ -100,13 +100,15 @@ def tile_picked_listconv_none_e_kernel(
                 else:
                     nc.scalar.activation(out=dst, in_=src, func=COPY)
 
-        def fill(c, h, part=slice(0, 4), engine_copy=on_vector):
+        def fill(c, h, part=None, engine_copy=on_vector):
+            part = part or slice(0, PHASES if c < LAST else RUNS)
             pair = slice(2 * h, 2 * h + 2)
             src = picked[h][:, :, c * CHUNK : (c + 1) * CHUNK]
             if c < LAST:
+                cols = slice(PACK * LANES * part.start, PACK * LANES * part.stop)
                 engine_copy(
-                    out=body[c][:].rearrange("p (r i e t) -> p i r e t", r=PHASES, e=2, t=PACK)[:, :, 4 * part.start : 4 * part.stop, :, pair],
-                    in_=src.rearrange("p u (i e r) -> p i r e u", e=2, r=PHASES)[:, :, 4 * part.start : 4 * part.stop],
+                    out=body[c][:, cols].rearrange("p (r i e t) -> p i r e t", i=LANES // 2, e=2, t=PACK)[:, :, :, :, pair],
+                    in_=src.rearrange("p u (i e r) -> p i r e u", e=2, r=PHASES)[:, :, part],
                 )
             else:
                 engine_copy(
@@ -211,27 +213,28 @@ def tile_picked_listconv_none_e_kernel(
         gather_row(2)
         open_banks()
         gather_row(3)
-        for c in range(CHUNKS):
-            if c == LAST:
-                fill_halo(1, on_scalar)
-            if c < LAST - 1:
-                fill(c, 1, slice(0, 2))
-                fill(c, 1, slice(2, 4))
-            else:
-                fill(c, 1)
-            if c == 0:
-                quantize(c, 0, HALF)
-                quantize(c, HALF, CHUNK)
-                for m in range(M_TILES):
-                    multiply(c, 0, HALF, (2, 1), False, (m,))
-                    multiply(c, HALF, CHUNK, (2, 1), False, (m,))
-                    multiply(c, 0, CHUNK, (0,), True, (m,))
-            elif c < LAST:
-                quantize(c)
-                multiply(c)
-            else:
-                quantize(c)
-                multiply(c)
-            if c > 0:
-                drain(c - 1)
+        fill(0, 1, slice(0, 8))
+        fill(0, 1, slice(8, 16))
+        quantize(0, 0, HALF)
+        multiply(0, 0, HALF, (2, 1, 0), False)
+        fill(1, 1, slice(0, 8))
+        fill(1, 1, slice(8, 16))
+        quantize(0, HALF, CHUNK)
+        multiply(0, HALF, CHUNK)
+        quantize(1)
+        multiply(1)
+        drain(0)
+        fill(2, 1, slice(0, 8))
+        fill(2, 1, slice(8, 16))
+        quantize(2, 0, HALF)
+        quantize(2, HALF, CHUNK)
+        multiply(2)
+        drain(1)
+        fill_halo(1, on_scalar)
+        fill(LAST, 1, slice(0, 1))
+        fill(LAST, 1, slice(1, 2))
+        fill(LAST, 1, slice(2, 4))
+        quantize(LAST)
+        multiply(LAST)
+        drain(LAST - 1)
         drain(LAST)

from contextlib import ExitStack

import concourse.mybir as mybir

K, T, S, N = 512, 2048, 1024, 256
TAPS = 3
FLOPS = 2 * TAPS * K * N * S

F32 = mybir.dt.float32
BF16 = mybir.dt.bfloat16
I32 = mybir.dt.int32
U16 = mybir.dt.uint16
U8 = mybir.dt.uint8
FP8X4 = mybir.dt.float8_e4m3fn_x4
ADD = mybir.AluOpType.add
COPY = mybir.ActivationFunctionType.Copy

P = 128
PACK = 4
LANES = 16
PHASES = 16
LINE = 4
CHUNK = LANES * PHASES
HALF = CHUNK // 2
OVER = TAPS - 1
CHUNKS = S // CHUNK
LAST = CHUNKS - 1
M_TILES = N // P
BANK = 512
RUN = 64
RUNS = CHUNK // RUN
HALO = OVER * RUN
OPENS = (((0, 128), (128, 256)), ((256, 256),), ((256, 128),))
OPEN_MAX = 256
GATHERS = (
    ((0, 512, "V"), (512, 1024, "S"),),
    ((0, 128, "V"), (128, 256, "S"), (256, 512, "S"), (512, 768, "S"), (768, 1024, "S"),),
    ((0, 320, "V"), (320, 1024, "S"),),
    ((0, 128, "V"), (128, 256, "S"), (256, 384, "V"), (384, 512, "S"), (512, 768, "S"), (768, 1024, "S"),),
)


def tile_picked_listconv_none_e_kernel(
    tc, xT, w1_words, w1_scales, w2_words, w2_scales, w3_words, w3_scales, offs, out
):
    nc = tc.nc
    with ExitStack() as ctx:
        keep = ctx.enter_context(tc.tile_pool(name="keep", bufs=1))
        psum = ctx.enter_context(tc.psum_pool(name="psum", bufs=1))
        on_scalar, on_vector = nc.scalar.copy, nc.vector.tensor_copy

        offsets = keep.tile([P, S // 16], U16, name="offsets")
        x_rows = xT.rearrange("(p j) t -> p j t", j=PACK)
        raw = [keep.tile([P, T], F32, name=f"raw{t}", tag=f"row{t}", align_bytes=64) for t in range(PACK)]
        weights = ((w1_words, w1_scales), (w2_words, w2_scales), (w3_words, w3_scales))
        planes = keep.tile([P, TAPS, N], U8, name="w_scales", align_bytes=64)
        nc.vector.memset(planes[:].rearrange("p d n -> p (d n)").bitcast(I32), 0)
        w_codes = [keep.tile([P, N], I32, name=f"w_codes{d}", align_bytes=64) for d in range(TAPS)]

        def load_row(t):
            nc.sync.dma_start(out=raw[t][:], in_=x_rows[:, t, :])

        def load_codes(d):
            nc.sync.dma_start(out=w_codes[d][:], in_=weights[d][0][0].rearrange("p n t -> p (n t)").bitcast(I32))

        load_row(0)
        nc.sync.dma_start(offsets[:], offs)
        load_row(1)
        for d in range(TAPS):
            nc.sync.dma_start(out=planes[98:100, d, :].bitcast(I32), in_=weights[d][1][0].bitcast(I32)[14:16, :])
        load_row(2)
        load_row(3)
        load_codes(2)
        for d in reversed(range(TAPS)):
            rows = weights[d][1][0].bitcast(I32)
            nc.sync.dma_start(
                out=planes[0:98, d, :].bitcast(I32), in_=rows[0:14, :].unsqueeze(0).to_broadcast([7, 14, N // 4])
            )
            if d < OVER:
                load_codes(d)

        width = [HALO + CHUNK if c == LAST else CHUNK for c in range(CHUNKS)]
        picked = [keep.tile([P, 2, S], BF16, name=f"picked{h}", tag=f"picked{h}", align_bytes=64) for h in range(2)]
        body = [keep.tile([P, PACK * width[c]], BF16, name=f"body{c}", tag=f"body{c}", align_bytes=64) for c in range(CHUNKS)]
        x_codes = {0: keep.tile([P, CHUNK + OPEN_MAX], I32, name="x_codes0", align_bytes=64)}
        x_scales = {}
        nc.vector.memset(x_codes[0][:, CHUNK:], 0)
        result = keep.tile([P, M_TILES, S], F32, name="result", align_bytes=64)
        results = [result[:, m, :] for m in range(M_TILES)]
        zeros = keep.tile([P, M_TILES, LINE], F32, name="zeros")
        nc.vector.memset(zeros[:], 0.0)
        nc.scalar.activation(out=result[:, :, 0:LINE], in_=zeros[:], func=COPY)

        def gather_row(t):
            for a, b, engine in GATHERS[t]:
                dst = picked[t // 2][:, t % 2, a:b]
                src = raw[t][:].indirect(offsets[:, a // 16 : b // 16])
                if engine == "V":
                    nc.vector.tensor_copy(out=dst, in_=src)
                else:
                    nc.scalar.activation(out=dst, in_=src, func=COPY)

        def fill(c, h, part=None, engine_copy=on_vector):
            part = part or slice(0, PHASES if c < LAST else RUNS)
            pair = slice(2 * h, 2 * h + 2)
            src = picked[h][:, :, c * CHUNK : (c + 1) * CHUNK]
            if c < LAST:
                cols = slice(PACK * LANES * part.start, PACK * LANES * part.stop)
                engine_copy(
                    out=body[c][:, cols].rearrange("p (r i e t) -> p i r e t", i=LANES // 2, e=2, t=PACK)[:, :, :, :, pair],
                    in_=src.rearrange("p u (i e r) -> p i r e u", e=2, r=PHASES)[:, :, part],
                )
            else:
                engine_copy(
                    out=body[c][:, PACK * HALO :].rearrange("p (r i e t) -> p i r e t", r=RUNS, e=2, t=PACK)[:, :, part, :, pair],
                    in_=src.rearrange("p u (i e r) -> p i r e u", e=2, r=RUNS)[:, :, part],
                )

        def fill_halo(h, engine_copy):
            pair = slice(2 * h, 2 * h + 2)
            back = picked[h][:, :, LAST * CHUNK - OVER : S - OVER]
            engine_copy(
                out=body[LAST][:, 0 : PACK * HALO].rearrange("p (r i e t) -> p i r e t", r=OVER, e=2, t=PACK)[:, :, :, :, pair],
                in_=back.rearrange("p u (i e r) -> p i r e u", e=2, r=RUNS)[:, :, 0:OVER],
            )

        out_rows = out.rearrange("(m p) s -> p m s", p=P)
        accs = [[psum.tile([P, BANK], F32, name=f"acc{c}_{m}") for m in range(M_TILES)] for c in range(CHUNKS)]

        def open_banks():
            x_scales[0] = keep.tile([P, CHUNK + OPEN_MAX], U8, name="x_scales0", tag="picked0", align_bytes=64)
            nc.vector.memset(x_scales[0][:, CHUNK:].bitcast(I32), 0)
            for c in range(LAST):
                for m in range(M_TILES):
                    for k, (at, n) in enumerate(OPENS[c]):
                        nc.tensor.matmul_mx(
                            out=accs[c][m][:, at : at + n],
                            lhsT=x_codes[0][:, CHUNK : CHUNK + P].bitcast(FP8X4),
                            lhsT_scale=x_scales[0][:, CHUNK : CHUNK + P],
                            rhs=x_codes[0][:, CHUNK : CHUNK + n].bitcast(FP8X4),
                            rhs_scale=x_scales[0][:, CHUNK : CHUNK + n],
                            start=(k == 0),
                            stop=False,
                        )

        def quantize(c, a=0, b=None):
            if c not in x_codes:
                x_codes[c] = keep.tile([P, width[c]], I32, name=f"x_codes{c}", tag=f"x_codes{c}", align_bytes=64)
                x_scales[c] = keep.tile([P, width[c]], U8, name=f"x_scales{c}", tag=f"x_scales{c}", align_bytes=64)
            b = width[c] if b is None else b
            nc.vector.quantize_mx(
                out=x_codes[c][:, a:b].bitcast(FP8X4), scales=x_scales[c][:, a:b], in_=body[c][:, PACK * a : PACK * b]
            )

        def multiply(c, a=0, b=CHUNK, taps=range(TAPS), closes=True, tiles=range(M_TILES)):
            for m in tiles:
                for d in taps:
                    src, dst = (0, d * LANES) if c < LAST else ((OVER - d) * RUN, 0)
                    m_cols = slice(m * P, (m + 1) * P)
                    nc.tensor.matmul_mx(
                        out=accs[c][m][:, dst + a : dst + b],
                        lhsT=w_codes[d][:, m_cols].bitcast(FP8X4),
                        lhsT_scale=planes[:, d, m_cols],
                        rhs=x_codes[c][:, src + a : src + b].bitcast(FP8X4),
                        rhs_scale=x_scales[c][:, src + a : src + b],
                        start=(c == LAST and a == 0 and d == 0),
                        stop=(closes and d == taps[-1]),
                    )

        def phases(c, m, r0, r1):
            return accs[c][m][:, r0 * LANES : r1 * LANES].rearrange("p (r i) -> p i r", i=LANES)

        def entries(c, m, r0, r1):
            col = c * CHUNK + r0
            return results[m][:, col : col + CHUNK].rearrange("p (i r) -> p i r", i=LANES)[:, :, 0 : r1 - r0]

        def leave(c, m, engine_copy):
            if c < LAST:
                engine_copy(
                    out=results[m][:, c * CHUNK + LINE : (c + 1) * CHUNK + LINE].rearrange("p (i q r) -> p q i r", i=LANES, r=LINE),
                    in_=accs[c][m][:, LINE * LANES : LINE * LANES + CHUNK].rearrange("p (q r i) -> p q i r", r=LINE, i=LANES),
                )
            else:
                engine_copy(
                    out=results[m][:, c * CHUNK : (c + 1) * CHUNK].rearrange("p (i r) -> p i r", r=RUNS),
                    in_=accs[c][m][:, 0:CHUNK].rearrange("p (r i) -> p i r", r=RUNS),
                )

        def join(c, m):
            sums = phases(c, m, 0, LINE)
            if (c, m) == (0, 0):
                firsts = keep.tile([P, LANES, LINE], F32, name="firsts", tag=f"x_scales{LAST}", align_bytes=64)
                on_scalar(out=firsts[:], in_=sums)
                sums = firsts[:]
            nc.vector.tensor_tensor(out=entries(c, m, 0, LINE), in0=sums, in1=entries(c, m, 0, LINE), op=ADD)

        def store(m, c0, c1):
            cols = slice(c0 * CHUNK, c1 * CHUNK)
            nc.sync.dma_start(out=out_rows[:, m, cols], in_=results[m][:, cols])

        def drain(c):
            for m in range(M_TILES):
                leave(c, m, on_vector if (c, m) == (LAST, 1) else on_scalar)
                if c < LAST:
                    join(c, m)
                store(m, c, c + 1)

        gather_row(0)
        gather_row(1)
        for c in range(CHUNKS):
            fill(c, 0)
        fill_halo(0, on_vector)
        gather_row(2)
        open_banks()
        gather_row(3)
        fill(0, 1, slice(0, 8))
        fill(0, 1, slice(8, 16))
        quantize(0, 0, HALF)
        multiply(0, 0, HALF, (2, 1, 0), False)
        fill(1, 1, slice(0, 8))
        fill(1, 1, slice(8, 16))
        quantize(0, HALF, CHUNK)
        multiply(0, HALF, CHUNK)
        quantize(1)
        multiply(1)
        drain(0)
        fill(2, 1, slice(0, 8))
        fill(2, 1, slice(8, 16))
        quantize(2, 0, HALF)
        quantize(2, HALF, CHUNK)
        multiply(2)
        drain(1)
        fill_halo(1, on_scalar)
        fill(LAST, 1, slice(0, 1))
        fill(LAST, 1, slice(1, 2))
        fill(LAST, 1, slice(2, 4))
        quantize(LAST)
        multiply(LAST)
        drain(LAST - 1)
        drain(LAST)
